import numpy as np, ml_dtypes
CORES = [242,247,114,119]
N = 4
BF = ml_dtypes.bfloat16
NL, W, B, RO, Q = 60, 1920, 112, 8, 2
def parts(rng):
    X = rng.integers(0, 256, (N, 8, 16, W)); L = rng.integers(0, W, (N, 8, 16, W))
    y = (rng.integers(0, 256, (N, 8, 16, B)) * rng.integers(1, 9, (N, 8, 1, B))) >> 3
    return X, L, y, rng.integers(0, NL, (N, 8, B)), rng.integers(0, 4096, (N, 8, B))
def pack(X, L, y, ln, T):
    return {"xw": np.ascontiguousarray(X.reshape(N, 128, W)).astype(np.float32).astype(BF), "il": np.ascontiguousarray(L.reshape(N, 128, W)).astype(np.int32),
            "y0": np.ascontiguousarray(y.reshape(N, 128, B)).astype(np.float32).astype(BF), "ln0": np.ascontiguousarray(ln).astype(np.int32), "tk0": np.ascontiguousarray(T).astype(np.int32)}
def setup_inputs(rng):
    return pack(*parts(rng))
def setup_inputs_spread(rng):
    X = rng.integers(0, 256, (N, 8, 16, W)) >> rng.integers(0, 9, (N, 8, 1, W)); y = rng.integers(0, 256, (N, 8, 16, B)) >> rng.integers(0, 9, (N, 8, 1, B))
    a = np.exp2(rng.integers(-2, 3, (N, 8, 16, 1))); b = np.exp2(rng.integers(-2, 3, (N, 8, 16, 1)))
    line = np.minimum((NL * rng.random((N, 8, 16, W)) ** a).astype(np.int64), NL - 1); wait = np.minimum((32 * rng.random((N, 8, 16, W)) ** b).astype(np.int64), 31)
    ln = np.minimum((NL * rng.random((N, 8, B)) ** 3).astype(np.int64), NL - 1); T = np.minimum(np.exp2(12 * rng.random((N, 8, B))).astype(np.int64) - 1, 4095)
    return pack(X, 32 * line + wait, y, ln, T)
def ends(rng, top, *shape):
    k = rng.integers(0, 4, shape[:-2] + (1, shape[-1]))
    return top * np.where(k < 2, k, rng.integers(0, 2, shape))
def setup_inputs_ends(rng):
    X = ends(rng, 255, N, 8, 16, W); y = ends(rng, 255, N, 8, 16, B)
    L = np.where(rng.random((N, 8, 16, W)) < 0.8, ends(rng, W - 1, N, 8, 16, W), rng.integers(0, W, (N, 8, 16, W)))
    ln = (NL - 1) * rng.integers(0, 2, (N, 8, B)); T = 4095 * rng.integers(0, 2, (N, 8, B))
    L[..., 0] = 0; L[:, :, 1, 0] = W - 1; L[..., 31] = (W - 1) * rng.integers(0, 2, (N, 8, 16))
    L[..., W - 32] = W - 1; L[:, :, 0, W - 32] = 0; L[..., W - 1] = W - 1; L[:, :, 0, W - 1] = 0
    X[..., 0] = 0; X[..., W - 1] = 0; X[..., W - 2] = 255
    for q in range(N):
        if q == 1:
            for c in (0, 31, W - 2, W - 1): X[q, :, :, c] = 255
            y[q] = np.where(np.argsort(rng.random((8, 16, B)), axis=1) < rng.integers(0, 9, (8, 1, B)), 0, 255)
        else:
            if q == N - 1: y[q] = 0
            for i, l, t, v in ((0, NL - 1, 4095, 0), (B - 1, NL - 1, 4095, 0), (B - 2, NL - 1, 4095, 255), (1, NL - 1, 0, 255), (B - 4, NL - 1, 0, 255), (3, 0, 0, 0), (B - 3, 0, 0, 0)):
                ln[q, :, i] = l; T[q, :, i] = t; y[q, :, :, i] = v
            if q == N - 1: y[q, :7, :, B - 2] = 0
            if q == 2: y[q] = np.where(np.argsort(rng.random((8, 16, B)), axis=1) < rng.integers(9, 17, (8, 1, B)), 0, 255)
    return pack(X, L, y, ln, T)
def setup_inputs_corners(rng):
    X, L, y, ln, T = parts(rng)
    T = np.where(rng.random(T.shape) < 0.7, rng.choice(np.array([0, 15, 16, 31, 32, 4064, 4080, 4095]), T.shape), T)
    ln = np.where(rng.random(ln.shape) < 0.4, rng.choice(np.array([0, NL - 1]), ln.shape), ln)
    for q in range(N):
        for g in range(8):
            e = (q + g) % 8
            if e == 0: ln[q, g] = ln[q, g, 0]; T[q, g] = T[q, g, B - 1]
            elif e == 1: L[q, g] = np.arange(W)
            elif e == 2: L[q, g] = 0
            elif e == 3: L[q, g] = W - 1
            elif e == 4: X[q, g] = np.maximum(X[q, g], 1); y[q, g] = np.where(np.argsort(rng.random((16, B)), axis=0) < rng.integers(8, 10, (1, B)), 0, 255)
            elif e == 5: X[q, g] = 0
            elif e == 6: X[q, g] = 255; y[q, g] = rng.integers(128, 256, (16, B))
            else:
                a = rng.permutation(W)[:B]; ln[q, g] = a >> 5; T[q, g] = (a & 31) + 32 * rng.integers(0, 128, B); h = B // 4
                pl = np.concatenate([np.array([0, W - 1]), 1 + rng.permutation(W - 2)])
                d = rng.permutation(np.concatenate([pl[:h], pl[:h], pl[h:B - h]]))
                L[q, g, 15, a] = (d & 4064) + ((d - T[q, g]) & 31)
    return pack(X, L, y, ln, T)
def setup_inputs_crowd(rng):
    X, L, y, ln, T = parts(rng)
    few = rng.integers(0, NL, (N, 8, 1, 4)); few[:, ::2, :, 0] = NL - 1; few[:, 1::2, :, 1] = 0
    L[:, :, 0:2] = (L[:, :, 0:2] & 31) + 32 * np.take_along_axis(few, rng.integers(0, 4, (N, 8, 1, 2 * W)), 3).reshape(N, 8, 2, W)
    L[:, :, 15:16] = (L[:, :, 15:16] & 31) + 32 * np.take_along_axis(few, rng.integers(0, 2, (N, 8, 1, W)), 3)
    ln = np.take_along_axis(few, rng.integers(0, 4, (N, 8, 1, B)), 3).reshape(N, 8, B)
    p = int(rng.integers(0, N)); q = (p + 1) % N
    X[p] = 0; y[p] = 255 - (rng.integers(0, 128, (8, 16, B)) >> (3 * rng.integers(0, 2, (8, 1, B))))
    X[q] = np.maximum(X[q], 1); y[q] = rng.integers(128, 256, (8, 16, B))
    y[q, int(rng.integers(0, 8)), :, rng.permutation(B)[:int(rng.integers(1, 32))]] = 0
    return pack(X, L, y, ln, T)
def check_inputs(d):
    bad = []
    for k, hi in (("xw", 255), ("il", W - 1), ("y0", 255), ("ln0", NL - 1), ("tk0", 4095)):
        v = np.asarray(d[k]).astype(np.float64)
        if not np.all((v >= 0) & (v <= hi)): bad.append("range of " + k)
        elif not np.all(v == np.floor(v)): bad.append("whole numbers of " + k)
    return bad
def reference(xw, il, y0, ln0, tk0):
    X = xw.astype(np.float32).astype(np.int64).reshape(N, 8, 16, W); L = il.astype(np.int64).reshape(N, 8, 16, W)
    y = y0.astype(np.float32).astype(np.int64).reshape(N, 8, 16, B); ln = ln0.astype(np.int64); T = tk0.astype(np.int64)
    A = np.zeros(N, np.int64)
    for step in range(RO):
        a = 32 * ln + (T & 31)
        c = np.take_along_axis(L, a[:, :, None, :], 3)
        s = (c & 4064) + ((c + T[:, :, None, :]) & 31)
        v = np.take_along_axis(X, np.ascontiguousarray(s.transpose(0, 1, 3, 2)).reshape(N, 8, 1, 16 * B), 3).reshape(N, 8, 16, B, 16 // Q, Q)
        m = np.max(np.min(v, axis=-1), axis=-1)
        z = np.abs(m - y)
        skip = np.add.reduce((z >= y).astype(np.int64), axis=2) >= 9
        ln = np.where(skip, c[:, :, 1], c[:, :, 0]) >> 5
        d = s[:, :, 15]
        T = (T + 1 + (np.add.reduce(z, axis=2) & 31) + (A & 31)[:, None, None]) & 4095
        A = np.add.reduce(skip.reshape(N, 8 * B).astype(np.int64), axis=1)
        y = np.roll(z, 1, axis=0); ln = np.roll(ln, 1, axis=0); T = np.roll(T, 1, axis=0); d = np.roll(d, 1, axis=0)
        for q in range(N):
            for g in range(8):
                p, first = np.unique(d[q, g], return_index=True)
                u = L[q, g]; o = u[:, p]
                u[:, p] = (o & 4064) + ((o + y[q, g][:, first]) & 31)
        if step < RO - 1:
            np.put_along_axis(X, (16 * np.arange(B) + (T & 15))[:, :, None, :], y, 3)
    return {"yw": (L & 31).reshape(N, 128, W).astype(np.float32).astype(BF), "yy": y.reshape(N, 128, B).astype(np.float32).astype(BF), "yl": ln.astype(np.float32), "yt": T.astype(np.float32)}

@@ -1,0 +1,497 @@
+from concourse.mybir import AluOpType as Op, ActivationFunctionType as Act
+
+NR, B, W, STEPS = 4, 112, 1920, 8
+BIG = float(3 * 2 ** 21)
+MAGIC = float(3 * 2 ** 27)
+CH = (0, 20, 48, 80, B)
+WT = W + B
+
+SCRATCH = {}
+for _names, _w, _t in (
+        ("xt lt", W, "bfloat16"), ("wt", WT, "bfloat16"), ("ili", W, "int32"), ("lf lg", W, "float32"),
+        ("tki lni ci cl ui u5 rz ry ft fu", B, "int32"),
+        ("t0f l0f mk1 qw uf fs fd fl fy fv", B, "float32"),
+        ("mkb iob wdm ge ge2 jk ug wf", B, "bfloat16"),
+        ("ip im pg mg p15 m15", 128, "int32"), ("idf e8f on32", 128, "float32"),
+        ("onf s15 idb nid gb gs se0 se1 nse onb", 128, "bfloat16"),
+        ("g8", 8, "bfloat16"), ("q16 ai aj", 8, "int32"), ("iw c1 cwn nb lose tp8 mn dl sk sd av", 8, "float32"), ("doff", 8, "uint16"),
+        ("acc af1 af2 q25", 1, "float32"), ("af", 4, "float32"),
+        ("qi tq", 16, "int32"), ("lbx ta", 16, "float32"), ("offs", 16, "uint16"),
+        ("r3 w3", 3 * B, "float32"), ("rd eq em", 7 * B, "bfloat16"),
+        ("r8", 8 * 44, "bfloat16"), ("vo mn2 mx", 8 * B, "bfloat16"), ("xr", B, "bfloat16"), ("sev sod", 56, "uint16"), ("nk", 8, "float32"),
+        ("elo ehi olo ohi", 128, "bfloat16"),
+        ("sall", 64, "float32"), ("si sj", 64, "int32"), ("pp pt tpa", 32, "float32"),
+        ("yb", 9 * 224, "bfloat16"),
+        ("lr", 8 * 224, "bfloat16"),
+        ("ey er", 8 * 224, "bfloat16"),
+        ("zo", 8 * B, "bfloat16"), ("eo", B, "float32"), ("flx k15", B, "bfloat16"), ("dof0", 8, "uint16")):
+    for _n in _names.split():
+        SCRATCH[_n] = ("sbuf", [128, _w], _t)
+PSUM = ["b%d" % i for i in range(8)]
+for _n in PSUM:
+    SCRATCH[_n] = ("psum", [128, 512], "float32")
+SEMAPHORES = ["sV", "sS", "sP", "sG", "lsem", "tp1", "tp2", "tp3"] + ["%s%d" % (a, i) for a in ("zr", "ea", "eb") for i in range(8)] + ["d%d" % i for i in range(16)]
+
+
+def rank_program(g, core, T, topo):
+    rank = T.rank_of(core)
+    if rank is None:
+        return
+    cores = T.cores
+    nxt, prv = cores[(rank + 1) % NR], cores[(rank - 1) % NR]
+    V, S, P = g.vector, g.scalar, g.tensor
+    queues = {"V": V, "S": S, "P": P, "G": g, "Y": g.sync}
+    sems = {"V": "sV", "S": "sS", "P": "sP", "G": "sG"}
+    cnt = {"V": 0, "S": 0, "P": 0, "G": 0}
+    know = {q: {} for q in queues}
+    clocks = {}
+    log = {}
+
+    def ensure(q, need):
+        need = {x: i for x, i in need.items() if know[q].get(x, 0) < i}
+        for x in list(need):
+            if any(y != x and clocks.get((y, j), {}).get(x, 0) >= need[x] for y, j in need.items()):
+                del need[x]
+        for x, i in need.items():
+            queues[q].wait_ge(T.sem[sems.get(x, x)], i)
+            for y, j in clocks.get((x, i), {}).items():
+                know[q][y] = max(know[q].get(y, 0), j)
+            know[q][x] = max(know[q].get(x, 0), i)
+
+    def deps(q, reads, writes):
+        need = {}
+        for regs, wr in ((reads, False), (writes, True)):
+            for name, a, b in regs:
+                ps = name in PSUM
+                for (c, d, x, i, w) in log.get(name, []):
+                    if x == q:
+                        if not (w and q != "P" and c < b and a < d):
+                            continue
+                    elif not (ps or (c < b and a < d and (w or wr))):
+                        continue
+                    need[x] = max(need.get(x, 0), i)
+        return need
+
+    def note(x, i, reads, writes):
+        for name, a, b in writes:
+            log[name] = [e for e in log.get(name, []) if not (a <= e[0] and e[1] <= b)] + [(a, b, x, i, True)]
+        for name, a, b in reads:
+            log[name] = [e for e in log.get(name, []) if e[4] or e[2] != x or not (a <= e[0] and e[1] <= b)] + [(a, b, x, i, False)]
+
+    def emit(q, reads, writes, fn):
+        ensure(q, deps(q, reads, writes))
+        fn().then_inc(T.sem[sems[q]], 1)
+        cnt[q] += 1
+        c = dict(know[q])
+        c[q] = cnt[q]
+        clocks[(q, cnt[q])] = c
+        note(q, cnt[q], reads, writes)
+
+    def R(name, a=0, b=None, st=1, p=None):
+        if b is None:
+            b = SCRATCH[name][1][1]
+        t = T[name]
+        if p is None:
+            ap = t[:, a:b] if st == 1 else t[:, a:b:st]
+        else:
+            ap = t[0:p, a:b] if st == 1 else t[0:p, a:b:st]
+        return (ap, [(name, a, b)], [])
+
+    def IND(win, off):
+        return (win[0].indirect(off[0]), win[1], off[1])
+
+    def rd(*ops):
+        return [r for o in ops if isinstance(o, tuple) for r in o[1] + o[2]]
+
+    def ap(o):
+        return o[0] if isinstance(o, tuple) else o
+
+    def tt(out, a, b, op):
+        emit("V", rd(a, b) + out[2], out[1], lambda: V.tensor_tensor(out=out[0], in0=a[0], in1=b[0], op=op))
+
+    def ts(out, a, s1, op0, s2=None, op1=None):
+        if op1 is None:
+            emit("V", rd(a, s1) + out[2], out[1], lambda: V.tensor_scalar(out=out[0], in0=a[0], scalar1=ap(s1), scalar2=None, op0=op0))
+        else:
+            emit("V", rd(a, s1, s2) + out[2], out[1], lambda: V.tensor_scalar(out=out[0], in0=a[0], scalar1=ap(s1), scalar2=ap(s2), op0=op0, op1=op1))
+
+    def cp(out, a):
+        emit("V", rd(a) + out[2], out[1], lambda: V.tensor_copy(out=out[0], in_=a[0]))
+
+    def scan(out, d0, d1, init, op0, op1):
+        emit("V", rd(d0, d1), out[1], lambda: V.tensor_tensor_scan(out=out[0], data0=d0[0], data1=d1[0], initial=init, op0=op0, op1=op1))
+
+    def fill(out, v):
+        emit("V", [], out[1], lambda: V.memset(out[0], v))
+
+    def act(out, a, f, bias=None, acc=None, scale=None):
+        kw = {}
+        if scale is not None:
+            kw["scale"] = scale
+        if bias is not None:
+            kw["bias"] = ap(bias)
+        if acc is not None:
+            kw["accum_out"] = acc[0]
+        emit("S", rd(a, bias), out[1] + (acc[1] if acc is not None else []),
+             lambda: S.activation(out=out[0], in_=a[0], func=f, **kw))
+
+    def mm(out, l, r, start, stop):
+        emit("P", rd(l, r), out[1], lambda: P.matmul(out[0], l[0], r[0], start, stop))
+
+    dma_all = []
+
+    def dma(q, out, src, reads, writes):
+        name = "d%d" % len(dma_all)
+        ensure(q, deps(q, reads, writes))
+        queues[q].dma_start(out=out, in_=src).then_inc(T.sem[name], 16)
+        c = dict(know[q])
+        c[name] = 16
+        clocks[(name, 16)] = c
+        note(name, 16, reads, writes)
+        dma_all.append(name)
+
+    sent = [0]
+
+    def send(dst, out, src, sem):
+        ensure("G", deps("G", src[1], []))
+        rid, pid = topo.addr(dst, core)
+        m = topo.mask(core, dst)
+        g.remote_dma(out_ap=out[0], in_ap=src[0], remote_sem=T.sem[sem], local_sem=T.sem.lsem, pid=pid, routing_id=rid, dma_engine_mask=m)
+        sent[0] += len(topo.engines(core, dst))
+
+    def landed(sem, src, regs):
+        note(sem, len(topo.engines(src, core)), [], regs)
+
+    dma("Y", T.tki[0:8, :], T.tk0[:, :], [], [("tki", 0, B)])
+    dma("S", T.lni[0:8, :], T.ln0[:, :], [], [("lni", 0, B)])
+    C4 = W // 4
+    for j in range(4):
+        dma("YS"[j % 2], T.ili[:, j * C4:(j + 1) * C4], T.il[:, j * C4:(j + 1) * C4], [], [("ili", j * C4, (j + 1) * C4)])
+    dma("S", T.xt[:, :], T.xw[:, :], [], [("xt", 0, W)])
+    dma("Y", T.yb[:, 0:B], T.y0[:, :], [], [("yb", 0, B)])
+
+    def iota(out, pat, base, cm, flag=False):
+        if flag:
+            emit("G", [], out[1], lambda: g.iota(out[0], pat, base, cm, allow_small_or_imprecise_dtypes=True))
+        else:
+            emit("G", [], out[1], lambda: g.iota(out[0], pat, base, cm))
+
+    def pick(out, ones, base, st=0):
+        emit("G", ones[1], out[1], lambda: g.affine_select(out=out[0], in_=ones[0], pattern=[[-16, 8], [st, 16]], compare_op=Op.is_equal,
+                                                           fill=0.0, base=base, channel_multiplier=1))
+    iota(R("ip"), [[0, 128]], 0, 1)
+    iota(R("im"), [[1, 128]], 0, 0)
+    fill(R("onb"), 1.0)
+    fill(R("r3"), float(2 ** 24))
+    fill(R("r3", 0, 3 * B, 16), 0.0)
+    pick(R("se0"), R("onb"), 0)
+    pick(R("se1"), R("onb"), -1)
+    fill(R("onf"), 256.0)
+    pick(R("s15"), R("onf"), -15)
+    tt(R("idb"), R("ip"), R("im"), Op.is_equal)
+    ts(R("mg"), R("im"), 4, Op.arith_shift_right)
+    ts(R("p15"), R("ip"), 15, Op.bitwise_and)
+    ts(R("m15"), R("im"), 15, Op.bitwise_and)
+    tt(R("e8f", p=8), R("ip", p=8), R("mg", p=8), Op.is_equal)
+    tt(R("mk1"), R("p15", 0, B), R("m15", 0, B), Op.is_equal)
+    cp(R("t0f", p=8), R("tki", p=8))
+    ts(R("l0f", p=8), R("lni", p=8), 32.0, Op.mult)
+    act(R("mkb"), R("mk1"), Act.Copy, scale=BIG)
+    act(R("nid"), R("idb"), Act.Copy, scale=-1.0)
+    act(R("idf"), R("idb"), Act.Copy)
+    act(R("nse"), R("se0"), Act.Copy, scale=-1.0)
+    P1, PQ, PZ, PL, PK, PW, P6, P7 = PSUM
+    E8 = R("e8f", p=8)
+    mm(R(P1, 0, B), E8, R("t0f", p=8), True, True)
+    fill(R("k15"), 15.5)
+    mm(R(PQ, 0, B), R("idb"), R("mkb"), True, False)
+    mm(R(PQ, 0, B), R("nid"), R("k15"), False, False)
+    mm(R(PQ, 0, B), E8, R("t0f", p=8), False, True)
+    mm(R(PW, B, 2 * B), R("idb"), R("mkb"), True, False)
+    mm(R(PW, B, 2 * B), E8, R("l0f", p=8), False, True)
+    fill(R("av"), 1.0)
+    fill(R("r8"), 255.0)
+    fill(R("r8", 0, 8 * 44, 8), 0.0)
+    ts(R("pg"), R("ip"), 4, Op.arith_shift_right)
+    tt(R("gb"), R("pg"), R("mg"), Op.is_equal)
+    for nm, base in (("elo", 0), ("ehi", 16), ("olo", -1), ("ohi", 15)):
+        pick(R(nm), R("gb"), base, -2)
+    act(R("gs"), R("gb"), Act.Copy, scale=float(2 ** 16))
+    fill(R("rd"), 0.0)
+    fill(R("rd", 0, 784, 112), 4096.0)
+    fill(R("eq"), 4096.0)
+    ts(R("q16"), R("im", 0, 8), 16, Op.mult)
+    tt(R("iw"), R("q16"), R("p15", 0, 8), Op.add)
+
+    def lines_of(j):
+        a, b = j * C4, (j + 1) * C4
+        ts(R("lf", a, b), R("ili", a, b), -15.5, Op.add)
+
+    def lines_act(j):
+        a, b = j * C4, (j + 1) * C4
+        act(R("lg", a, b), R("lf", a, b), Act.Identity, MAGIC)
+        act(R("lt", a, b), R("lg", a, b), Act.Identity, -MAGIC)
+
+    def waits_of(j):
+        a, b = j * C4, (j + 1) * C4
+        bank = (PW, PL, PZ, PQ)[j]
+        mm(R(bank, 0, C4), R("idb"), R("lt", a, b), True, True)
+        tt(R("wt", a, b), R("ili", a, b), R(bank, 0, C4), Op.subtract)
+
+    SEG = lambda name, k=0: R(name, k * B + 15, (k + 1) * B, 16)
+    S7 = lambda name: R(name, 0, 7)
+
+    def parts_of(n):
+        m0, m1 = (0, 3) if n == 6 else (3, 4)
+        hi = n + 1
+        cp(R("si", 0, 8 * hi, p=B), R("sall", 0, 8 * hi, p=B))
+        ts(R("ai", 0, hi), R("av", 0, hi), -1.0, Op.add)
+        ts(R("sj", 0, 8 * hi, p=B), R("si", 0, 8 * hi, p=B), 31, Op.bitwise_and)
+        ts(R("aj", 0, hi), R("ai", 0, hi), 31, Op.bitwise_and)
+        tt(R("pp", 8 * m0, 8 * m1, p=B), R("sj", 8 * m0, 8 * m1, p=B), R("sj", 8 * m0 + 32, 8 * m1 + 32, p=B), Op.add)
+        tt(R("af", m0, m1), R("aj", m0, m1), R("aj", m0 + 4, m1 + 4), Op.add)
+        if n == 6:
+            fill(R("pt"), 0.0)
+        for j in range(m0, m1):
+            ts(R("pt", 8 * j, 8 * j + 8, p=B), R("pp", 8 * j, 8 * j + 8, p=B), R("af", j, j + 1, p=B), Op.add, 2.0, Op.add)
+            if j > 0:
+                send(cores[(rank - j) % NR], R("tpa", 8 * j, 8 * j + 8), R("pt", 8 * j, 8 * j + 8), "tp%d" % j)
+
+    def tail_of(n):
+        if n < 7:
+            act(R("af1"), R(P7, 256, 257), Act.Identity, MAGIC)
+            act(R("af2"), R("af1"), Act.Identity, MAGIC, scale=-1.0)
+            act(R("av", n + 1, n + 2), R(P7, 256, 257), Act.Identity, R("af2"))
+        if n >= 6:
+            parts_of(n)
+
+    for n in range(STEPS + 1):
+        last = n == STEPS
+        y0 = 224 * n
+        z, clk = R("yb", y0, y0 + B), R("yb", y0 + B, y0 + 2 * B)
+        lns, rot = (None, None) if last else (R("lr", y0, y0 + B), R("lr", y0 + B, y0 + 2 * B))
+        if n > 0:
+            k = n - 1
+            e0 = 224 * k
+            ey, ec = R("ey", e0, e0 + B), R("ey", e0 + B, e0 + 2 * B)
+            el, et = R("er", e0, e0 + B), R("er", e0 + B, e0 + 2 * B)
+            landed("ea%d" % k, prv, [("ey", e0, e0 + (224 if k < 7 else 112))])
+            landed("eb%d" % k, prv, [("er", e0, e0 + 224)])
+            KM = R(P6, 256, 256 + B)
+            mm(KM, R("s15"), el, False, False)
+            mm(KM, R("s15"), et, False, True)
+            mm(R(PK, 0, B), R("s15"), el, False, False)
+            mm(R(PK, 0, B), R("s15"), et, False, True)
+            if not last:
+                mm(R(P7, B, 2 * B), R("gb"), R("ge2"), True, True)
+            for c in (0, B):
+                mm(R(PW, c, c + B), R("idb"), R("mkb"), True, False)
+                if c:
+                    mm(R(PW, c, c + B), R("se1"), el, False, False)
+                mm(R(PW, c, c + B), R("nse" if c else "se0"), el, False, True)
+            mm(R(PZ, 0, B), R("nid"), ey, True, False)
+            if not last:
+                mm(R(PQ, 0, B), R("idb"), R("mkb"), True, False)
+                mm(R(PQ, 0, B), R("nid"), R("k15"), False, False)
+                mm(R(PQ, 0, B), R("idb"), ec, False, False)
+                mm(R(P1, 0, B), R("idb"), ec, True, False)
+                UC = R(P7, 280, 280 + B)
+                PX, PE, PO, PR = R(PW, 256, 256 + B), R(PL, 0, 56), R(PZ, 128, 184), R(P6, 128, 128 + B)
+            scan(R("w3", 0, B), R("r3", 0, B), KM, 0.0, Op.min, Op.max)
+            tt(S7("nb"), S7("c1"), SEG("w3"), Op.subtract)
+            for q in range(7):
+                L = 16 * q + 16
+                act(R("eq", 112 * q + 112 - L, 112 * q + 112), R(PK, 0, L), Act.Abs, R("nb", q, q + 1))
+            ts(S7("dof0"), S7("nb"), -1.0 / 256, Op.mult)
+            ts(S7("nk"), S7("nb"), 2.0 ** -20, Op.mult)
+            ts(R("wdm"), IND(R("wt"), S7("dof0")), -32.0, Op.add)
+            tt(S7("nk"), S7("nk"), S7("iw"), Op.subtract)
+            scan(R("em", 0, 448), R("rd", 0, 448), R("eq", 0, 448), 4096.0, Op.max, Op.min)
+            scan(R("em", 448, 784), R("rd", 448, 784), R("eq", 448, 784), 4096.0, Op.max, Op.min)
+            scan(R("w3", B, 3 * B), R("r3", B, 3 * B), R(PW, 0, 2 * B), 0.0, Op.min, Op.max)
+            tt(S7("tp8"), R("em", 111, 784, 112), S7("nk"), Op.add)
+            ts(S7("dl"), SEG("w3", 2), -BIG, Op.add)
+            ts(S7("lbx"), SEG("w3", 1), -BIG, Op.add)
+            tt(S7("mn"), S7("tp8"), S7("cwn"), Op.max)
+            ts(S7("doff"), S7("mn"), -4096.0, Op.mult)
+            if last:
+                mm(R(P6, 0, B), R("se0"), el, True, True)
+                mm(R(P6, B, 2 * B), R("se1"), el, True, False)
+                mm(R(P6, B, 2 * B), R("nse"), el, False, True)
+            if not last:
+                act(R("jk"), R(P7, B, 2 * B), Act.Sign, -1.0, R("acc"))
+                mm(R(P7, 256, 257), R("on32"), R("q25"), True, False)
+                mm(R(P7, 256, 257), R("on32"), R("acc"), False, True)
+                if n == 7:
+                    tail_of(k)
+            landed("zr%d" % k, prv, z[1])
+            mm(R(PZ, 0, B), R("idb"), z, False, True)
+            if not last:
+                mm(R(PQ, 0, B), R("gb"), z, False, False)
+                mm(R(P1, 0, B), R("gb"), z, False, True)
+                tt(IND(R("wt"), S7("doff")), R("wdm"), z, Op.add)
+            act(R("ge"), R(PZ, 0, B), Act.Sign, 0.5)
+            mm(R(PQ, 0, B), R("gb" if last else "gs"), R("ge"), last, True)
+            if not last:
+                mm(UC, R("idb"), ec, True, False)
+                mm(UC, R("gb"), z, False, False)
+                mm(PX, R("idb"), R("k15"), True, False)
+        if last:
+            break
+        scan(R("qw"), R("r3", 0, B), R(PQ, 0, B), 0.0, Op.min, Op.max)
+        if n == 0:
+            scan(R("w3", B, 2 * B), R("r3", B, 2 * B), R(PW, B, 2 * B), 0.0, Op.min, Op.max)
+            ts(S7("lbx"), SEG("w3", 1), -BIG, Op.add)
+        tt(S7("ta"), SEG("qw"), S7("lbx"), Op.add)
+        if n > 0:
+            ts(S7("sk"), SEG("qw"), BIG + 2.0 ** 16, Op.is_ge)
+        ts(S7("mn"), SEG("qw"), MAGIC, Op.add, -MAGIC, Op.add)
+        if n > 0:
+            ts(S7("qi"), SEG("qw"), 15.5, Op.add)
+            tt(S7("sd"), S7("sk"), S7("dl"), Op.mult)
+        tt(S7("ta"), S7("ta"), S7("mn"), Op.subtract)
+        if n > 0:
+            ts(S7("tq"), S7("qi"), 15, Op.bitwise_and)
+            tt(S7("ta"), S7("ta"), S7("sd"), Op.add)
+            tt(R("ta", 8, 15), S7("tq"), R("lbx", 8, 15), Op.add)
+        ts(S7("offs"), S7("ta"), 15.5, Op.add)
+        if n > 0:
+            cp(R("offs", 8, 15), R("ta", 8, 15))
+        act(R("uf"), R(P1, 0, B), Act.Identity, MAGIC)
+        act(R("ug"), R("uf"), Act.Identity, -MAGIC)
+        if n == 0:
+            UC = R(P7, 280, 280 + B)
+            mm(UC, E8, R("t0f", p=8), True, False)
+        mm(UC, R("nid"), R("ug"), False, True)
+        if n > 0:
+            act(R("xr"), UC, Act.Copy)
+        if n > 0:
+            act(R("wf"), IND(R("wt"), S7("offs")), Act.Copy)
+            act(lns, IND(R("lt"), S7("offs")), Act.Copy)
+            if n < 7:
+                tail_of(n - 1)
+        if n < 7:
+            act(clk, UC, Act.Identity, R("av", n, n + 1))
+        if n > 0:
+            cp(IND(R("xt"), R("offs", 8, 15)), z)
+            lists = ((PO, "olo", "ohi"), (PE, "elo", "ehi"))
+
+            def halves(pb, lo, hi, name, a, start, stop):
+                mm(pb, R(lo), R(name, a, a + B, 2), start, False)
+                mm(pb, R(hi), R(name, a + 1, a + B, 2), False, stop)
+            for pb, lo, hi in lists:
+                halves(pb, lo, hi, "xr", 0, True, False)
+            mm(PR, R("idb"), R("xr"), True, False)
+            mm(PX, R("nid"), R("xr"), False, False)
+            mm(PX, R("nid"), R("wf"), False, True)
+            ts(R("flx"), PX, MAGIC, Op.add, -MAGIC, Op.add)
+            halves(PO, "olo", "ohi", "wf", 0, False, False)
+            halves(PO, "olo", "ohi", "lr", y0, False, False)
+            halves(PO, "olo", "ohi", "flx", 0, False, True)
+            mm(PR, R("idb"), R("wf"), False, False)
+            mm(PR, R("idb"), R("flx"), False, True)
+            halves(PE, "elo", "ehi", "wf", 0, False, False)
+            halves(PE, "elo", "ehi", "lr", y0, False, False)
+            halves(PE, "elo", "ehi", "flx", 0, False, True)
+            tt(R("rz"), R("wdm"), z, Op.add)
+            cp(R("sod"), PO)
+            ts(R("ry"), R("rz"), 31, Op.bitwise_and)
+            cp(R("sev"), PE)
+        else:
+            fill(R("wt", W, WT), 0.0)
+            fill(R("q25"), 0.25)
+            fill(R("on32"), 1.0 / 32)
+            cp(R("iob"), R("im", 0, B))
+            tt(R("g8"), R("pg", 0, 8), R("im", 0, 8), Op.is_equal)
+            ts(S7("c1"), S7("iw"), BIG, Op.add)
+            ts(S7("cwn"), S7("iw"), -1.0 / 4096, Op.mult, -W / 4096.0, Op.add)
+            ts(R("lbx", 8, 15), S7("iw"), 16.0, Op.mult)
+            for j in range(3):
+                lines_of(j)
+                lines_act(j)
+            cp(R("ci"), IND(R("ili"), S7("offs")))
+            tt(R("ui"), R("ci"), R(P1, 0, B), Op.add)
+            ts(R("cl"), R("ci"), 4064, Op.bitwise_and)
+            ts(R("u5"), R("ui"), 31, Op.bitwise_and)
+            cp(lns, R("cl"))
+            cp(rot, R("u5"))
+            for pb, lo, hi, od in ((R(PZ, 128, 184), "olo", "ohi", "sod"), (R(PL, 0, 56), "elo", "ehi", "sev")):
+                for o in (0, B):
+                    mm(pb, R(lo), R("lr", o, o + B, 2), o == 0, False)
+                    mm(pb, R(hi), R("lr", o + 1, o + B, 2), False, o > 0)
+                cp(R(od), pb)
+            lines_of(3)
+            waits_of(0)
+        if n > 0:
+            act(rot, PR, Act.Copy)
+        for a, b in zip(CH, CH[1:]):
+            act(R("vo", 8 * a, 8 * b), IND(R("xt"), R("sod", a // 2, b // 2)), Act.Copy)
+            if a == 0:
+                send(nxt, R("er", y0, y0 + 224), R("lr", y0, y0 + 224), "eb%d" % n)
+                ew = 224 if n < 7 else 112
+                send(nxt, R("ey", y0, y0 + ew), R("yb", y0, y0 + ew), "ea%d" % n)
+        M = CH[-3]
+        mm(R(PK, 0, M), R("nid"), R("yb", y0, y0 + M), True, False)
+        mm(R(P6, 0, B - M), R("nid"), R("yb", y0 + M, y0 + B), True, False)
+
+        def least(k):
+            a, b = CH[k], CH[k + 1]
+            tt(R("mn2", 8 * a, 8 * b), IND(R("xt"), R("sev", a // 2, b // 2)), R("vo", 8 * a, 8 * b), Op.min)
+
+        def greatest(a, b):
+            scan(R("mx", 8 * a, 8 * b), R("r8", 0, 8 * (b - a)), R("mn2", 8 * a, 8 * b), 0.0, Op.min, Op.max)
+        for k in range(len(CH) - 1):
+            least(k)
+            if k > 0:
+                greatest(CH[k - 1], CH[k])
+        greatest(CH[-2], B)
+        zo = B * n
+        mm(R(PK, 0, M), R("idb"), R("mx", 7, 8 * M, 8), False, True)
+        mm(R(P6, 0, B - M), R("idb"), R("mx", 8 * M + 7, 8 * B, 8), False, True)
+        act(R("zo", zo, zo + M), R(PK, 0, M), Act.Abs)
+        act(R("zo", zo + M, zo + B), R(P6, 0, B - M), Act.Abs)
+        zo = R("zo", zo, zo + B)
+        send(nxt, R("yb", y0 + 224, y0 + 224 + B), zo, "zr%d" % n)
+        if n > 0:
+            cp(IND(R("wt"), S7("doff")), R("ry"))
+        KM = R(P6, 256, 256 + B)
+        mm(KM, R("idb"), R("mkb"), True, False)
+        mm(KM, R("idb"), R("iob"), False, False)
+        mm(R(PK, 0, B), R("idb"), R("iob"), True, False)
+        if n == 0:
+            lines_act(3)
+            for j in range(1, 4):
+                waits_of(j)
+        if n < 7:
+            mm(R(P7, 0, B), R("nid"), z, True, False)
+            mm(R(P7, 0, B), R("idb"), zo, False, True)
+            act(R("ge2"), R(P7, 0, B), Act.Sign, 0.5)
+        mm(R(PL, 264, 272, p=B), zo, R("g8"), True, True)
+        act(R("sall", 8 * n, 8 * n + 8, p=B), R(PL, 264, 272, p=B), Act.Copy)
+        if n == 7:
+            tail_of(n)
+
+    tt(R("rz"), R("wdm"), z, Op.add)
+    ts(R("ry"), R("rz"), 31, Op.bitwise_and)
+    cp(IND(R("wt"), S7("doff")), R("ry"))
+    dma("Y", T.yw[:, :], T.wt[:, 0:W], [("wt", 0, W)], [])
+    dma("S", T.yy[:, :], T.yb[:, y0:y0 + B], z[1], [])
+    ts(R("fs"), R(PQ, 0, B), 1.0, Op.is_ge)
+    tt(R("fd"), R("fs"), R(P6, B, 2 * B), Op.mult)
+    tt(R("fl"), R("fd"), R(P6, 0, B), Op.add)
+    ts(R("fy"), R("fl"), 1.0 / 32, Op.mult)
+    dma("S", T.yl[:, :], T.fy[0:128:16, :], [("fy", 0, B)], [])
+    for j in range(1, 4):
+        landed("tp%d" % j, cores[(rank + j) % NR], [("tpa", 8 * j, 8 * j + 8)])
+    idq = (T.idf[0:B, 0:B], [("idf", 0, B)], [])
+    for j in range(4):
+        mm(R(P1, 0, B, p=8), R("pt" if j == 0 else "tpa", 8 * j, 8 * j + 8, p=B), idq, j == 0, j == 3)
+    tt(R("ft", p=8), R("tki", p=8), R(P1, 0, B, p=8), Op.add)
+    ts(R("fu", p=8), R("ft", p=8), 4095, Op.bitwise_and)
+    cp(R("fv", p=8), R("fu", p=8))
+    dma("Y", T.yt[:, :], T.fv[0:8, :], [("fv", 0, B)], [])
+    for q in ("V", "S", "P", "G"):
+        g.wait_ge(T.sem[sems[q]], cnt[q])
+    for name in dma_all:
+        g.wait_ge(T.sem[name], 16)
+    g.wait_ge(T.sem.lsem, sent[0])

@@ -1,36 +1,40 @@
 from concourse.mybir import AluOpType as Op, ActivationFunctionType as Act
 
 NR, B, W, STEPS = 4, 112, 1920, 8
-BIG = float(3 * 2 ** 21)
-MAGIC = float(3 * 2 ** 27)
-CH = (0, 20, 48, 80, B)
+OFF = float(2 ** 23)
+M16, M32 = float(3 * 2 ** 26), float(3 * 2 ** 27)
+LO = 6144.0
+C0 = 2 * LO - 15.5
+HI = 8192.0
+CH = (0, 8, 28, 56, 88, B)
+SC = (0, 28, 56, 88, B)
+EARLY = 56
+IL = (0, 480, 960, 1440, W)
 WT = W + B
+P0 = 89
 
 SCRATCH = {}
 for _names, _w, _t in (
-        ("xt lt", W, "bfloat16"), ("wt", WT, "bfloat16"), ("ili", W, "int32"), ("lf lg", W, "float32"),
-        ("tki lni ci cl ui u5 rz ry ft fu", B, "int32"),
-        ("t0f l0f mk1 qw uf fs fd fl fy fv", B, "float32"),
-        ("mkb iob wdm ge ge2 jk ug wf", B, "bfloat16"),
-        ("ip im pg mg p15 m15", 128, "int32"), ("idf e8f on32", 128, "float32"),
-        ("onf s15 idb nid gb gs se0 se1 nse onb", 128, "bfloat16"),
-        ("g8", 8, "bfloat16"), ("q16 ai aj", 8, "int32"), ("iw c1 cwn nb lose tp8 mn dl sk sd av", 8, "float32"), ("doff", 8, "uint16"),
-        ("acc af1 af2 q25", 1, "float32"), ("af", 4, "float32"),
-        ("qi tq", 16, "int32"), ("lbx ta", 16, "float32"), ("offs", 16, "uint16"),
-        ("r3 w3", 3 * B, "float32"), ("rd eq em", 7 * B, "bfloat16"),
-        ("r8", 8 * 44, "bfloat16"), ("vo mn2 mx", 8 * B, "bfloat16"), ("xr", B, "bfloat16"), ("sev sod", 56, "uint16"), ("nk", 8, "float32"),
-        ("elo ehi olo ohi", 128, "bfloat16"),
-        ("sall", 64, "float32"), ("si sj", 64, "int32"), ("pp pt tpa", 32, "float32"),
-        ("yb", 9 * 224, "bfloat16"),
-        ("lr", 8 * 224, "bfloat16"),
-        ("ey er", 8 * 224, "bfloat16"),
-        ("zo", 8 * B, "bfloat16"), ("eo", B, "float32"), ("flx k15", B, "bfloat16"), ("dof0", 8, "uint16")):
+        ("xt", W, "bfloat16"), ("wt", WT, "bfloat16"), ("ili an", W, "int32"),
+        ("tki lni ui u5 rz ry ft fu", B, "int32"), ("ip", 8, "int32"), ("p15", 8, "int32"),
+        ("km fy fv", B, "float32"), ("pf ac", 8, "float32"), ("i16", 32, "float32"),
+        ("t5b l32 fm fm8 xr wdb ge sg fx r3 fs fd fl", B, "bfloat16"),
+        ("va vb vc ve e8 vf onb neg f16 idb nid gb gp gn se0 se1 sd s15 elo ehi olo ohi", 128, "bfloat16"),
+        ("iw cwn nk tp8 mn av am jk", 16, "float32"), ("fa fz", 8, "bfloat16"),
+        ("doff dof0", 8, "uint16"), ("o0", 16, "uint16"), ("idl", 32, "uint16"), ("sev sod", 56, "uint16"),
+        ("rd eq em", 7 * B, "bfloat16"), ("r8", 8 * 32, "bfloat16"), ("vo mn2 mx", 8 * B, "bfloat16"),
+        ("pb", 880, "float32"), ("da db", 64, "bfloat16"), ("ob", B, "float32"),
+        ("zi", 9 * B, "bfloat16"), ("zo", 8 * B, "bfloat16"),
+        ("mo mi", 8 * 4 * B, "bfloat16"),
+        ("oo oi", 8 * 16, "uint16"),
+        ("dt di", 64 + B, "bfloat16")):
     for _n in _names.split():
         SCRATCH[_n] = ("sbuf", [128, _w], _t)
 PSUM = ["b%d" % i for i in range(8)]
 for _n in PSUM:
     SCRATCH[_n] = ("psum", [128, 512], "float32")
-SEMAPHORES = ["sV", "sS", "sP", "sG", "lsem", "tp1", "tp2", "tp3"] + ["%s%d" % (a, i) for a in ("zr", "ea", "eb") for i in range(8)] + ["d%d" % i for i in range(16)]
+SEMAPHORES = (["sV", "sS", "sP", "sG", "lsem", "ck", "tp1", "tp2", "tp3"] + ["%s%d" % (a, i) for a in ("zr", "ea", "of") for i in range(8)]
+              + ["d%d" % i for i in range(16)])
 
 
 def rank_program(g, core, T, topo):
@@ -61,22 +65,22 @@ def rank_program(g, core, T, topo):
     def deps(q, reads, writes):
         need = {}
         for regs, wr in ((reads, False), (writes, True)):
-            for name, a, b in regs:
+            for name, cols in regs:
                 ps = name in PSUM
-                for (c, d, x, i, w) in log.get(name, []):
+                for (c, x, i, w) in log.get(name, []):
                     if x == q:
-                        if not (w and q != "P" and c < b and a < d):
+                        if not (w and q != "P" and c & cols):
                             continue
-                    elif not (ps or (c < b and a < d and (w or wr))):
+                    elif not (ps or (c & cols and (w or wr))):
                         continue
                     need[x] = max(need.get(x, 0), i)
         return need
 
     def note(x, i, reads, writes):
-        for name, a, b in writes:
-            log[name] = [e for e in log.get(name, []) if not (a <= e[0] and e[1] <= b)] + [(a, b, x, i, True)]
-        for name, a, b in reads:
-            log[name] = [e for e in log.get(name, []) if e[4] or e[2] != x or not (a <= e[0] and e[1] <= b)] + [(a, b, x, i, False)]
+        for name, cols in writes:
+            log[name] = [e for e in log.get(name, []) if e[0] & ~cols] + [(cols, x, i, True)]
+        for name, cols in reads:
+            log[name] = [e for e in log.get(name, []) if e[3] or e[1] != x or e[0] & ~cols] + [(cols, x, i, False)]
 
     def emit(q, reads, writes, fn):
         ensure(q, deps(q, reads, writes))
@@ -87,15 +91,12 @@ def rank_program(g, core, T, topo):
         clocks[(q, cnt[q])] = c
         note(q, cnt[q], reads, writes)
 
-    def R(name, a=0, b=None, st=1, p=None):
+    def R(name, a=0, b=None, st=1, p=128):
         if b is None:
             b = SCRATCH[name][1][1]
         t = T[name]
-        if p is None:
-            ap = t[:, a:b] if st == 1 else t[:, a:b:st]
-        else:
-            ap = t[0:p, a:b] if st == 1 else t[0:p, a:b:st]
-        return (ap, [(name, a, b)], [])
+        cols = (1 << b) - (1 << a) if st == 1 else sum(1 << c for c in range(a, b, st))
+        return (t[0:p, a:b] if st == 1 else t[0:p, a:b:st], [(name, cols)], [])
 
     def IND(win, off):
         return (win[0].indirect(off[0]), win[1], off[1])
@@ -138,6 +139,12 @@ def rank_program(g, core, T, topo):
     def mm(out, l, r, start, stop):
         emit("P", rd(l, r), out[1], lambda: P.matmul(out[0], l[0], r[0], start, stop))
 
+    def iota(out, pat, base, cm):
+        if SCRATCH[out[1][0][0]][2] == "int32":
+            emit("G", [], out[1], lambda: g.iota(out[0], pat, base, cm))
+        else:
+            emit("G", [], out[1], lambda: g.iota(out[0], pat, base, cm, allow_small_or_imprecise_dtypes=True))
+
     dma_all = []
 
     def dma(q, out, src, reads, writes):
@@ -155,341 +162,297 @@ def rank_program(g, core, T, topo):
     def send(dst, out, src, sem):
         ensure("G", deps("G", src[1], []))
         rid, pid = topo.addr(dst, core)
-        m = topo.mask(core, dst)
-        g.remote_dma(out_ap=out[0], in_ap=src[0], remote_sem=T.sem[sem], local_sem=T.sem.lsem, pid=pid, routing_id=rid, dma_engine_mask=m)
+        g.remote_dma(out_ap=out[0], in_ap=src[0], remote_sem=T.sem[sem], local_sem=T.sem.lsem, pid=pid, routing_id=rid,
+                     dma_engine_mask=topo.mask(core, dst))
         sent[0] += len(topo.engines(core, dst))
 
-    def landed(sem, src, regs):
-        note(sem, len(topo.engines(src, core)), [], regs)
+    def landed(sem, src, reg):
+        note(sem, len(topo.engines(src, core)), [], reg[1])
 
-    dma("Y", T.tki[0:8, :], T.tk0[:, :], [], [("tki", 0, B)])
-    dma("S", T.lni[0:8, :], T.ln0[:, :], [], [("lni", 0, B)])
-    C4 = W // 4
+    BQ, BL, BK, BP, BO, BE, BX, BS = PSUM
+    S7 = lambda name: R(name, 0, 7)
+    SEG = R("km", 15, B, 16)
+    slot = lambda k, q0=0: R("pb", P0 + 16 * k + B * q0, P0 + 16 * k + B * (q0 + 6) + 1, B)
+    into = lambda k: R("pb", P0 + 16 * k - 105, P0 + 16 * k - 105 + 7 * B, 7)
+    F16, FM, FM8 = R("f16", p=16), R("fm", p=16), R("fm8", p=16)
+
+    def turn(out, src):
+        scan(out, R("r3"), src, 0.0, Op.min, Op.max)
+
+    dma("Y", T.tki[0:8, :], T.tk0[:, :], [], R("tki")[1])
+    dma("S", T.lni[0:8, :], T.ln0[:, :], [], R("lni")[1])
     for j in range(4):
-        dma("YS"[j % 2], T.ili[:, j * C4:(j + 1) * C4], T.il[:, j * C4:(j + 1) * C4], [], [("ili", j * C4, (j + 1) * C4)])
-    dma("S", T.xt[:, :], T.xw[:, :], [], [("xt", 0, W)])
-    dma("Y", T.yb[:, 0:B], T.y0[:, :], [], [("yb", 0, B)])
+        a, b = IL[j], IL[j + 1]
+        dma("Y", T.ili[:, a:b], T.il[:, a:b], [], R("ili", a, b)[1])
+    dma("Y", T.xt[:, :], T.xw[:, :], [], R("xt")[1])
+    dma("Y", T.zi[:, 0:B], T.y0[:, :], [], R("zi", 0, B)[1])
 
-    def iota(out, pat, base, cm, flag=False):
-        if flag:
-            emit("G", [], out[1], lambda: g.iota(out[0], pat, base, cm, allow_small_or_imprecise_dtypes=True))
-        else:
-            emit("G", [], out[1], lambda: g.iota(out[0], pat, base, cm))
-
-    def pick(out, ones, base, st=0):
-        emit("G", ones[1], out[1], lambda: g.affine_select(out=out[0], in_=ones[0], pattern=[[-16, 8], [st, 16]], compare_op=Op.is_equal,
-                                                           fill=0.0, base=base, channel_multiplier=1))
-    iota(R("ip"), [[0, 128]], 0, 1)
-    iota(R("im"), [[1, 128]], 0, 0)
-    fill(R("onb"), 1.0)
-    fill(R("r3"), float(2 ** 24))
-    fill(R("r3", 0, 3 * B, 16), 0.0)
-    pick(R("se0"), R("onb"), 0)
-    pick(R("se1"), R("onb"), -1)
-    fill(R("onf"), 256.0)
-    pick(R("s15"), R("onf"), -15)
-    tt(R("idb"), R("ip"), R("im"), Op.is_equal)
-    ts(R("mg"), R("im"), 4, Op.arith_shift_right)
-    ts(R("p15"), R("ip"), 15, Op.bitwise_and)
-    ts(R("m15"), R("im"), 15, Op.bitwise_and)
-    tt(R("e8f", p=8), R("ip", p=8), R("mg", p=8), Op.is_equal)
-    tt(R("mk1"), R("p15", 0, B), R("m15", 0, B), Op.is_equal)
-    cp(R("t0f", p=8), R("tki", p=8))
-    ts(R("l0f", p=8), R("lni", p=8), 32.0, Op.mult)
-    act(R("mkb"), R("mk1"), Act.Copy, scale=BIG)
-    act(R("nid"), R("idb"), Act.Copy, scale=-1.0)
-    act(R("idf"), R("idb"), Act.Copy)
-    act(R("nse"), R("se0"), Act.Copy, scale=-1.0)
-    P1, PQ, PZ, PL, PK, PW, P6, P7 = PSUM
-    E8 = R("e8f", p=8)
-    mm(R(P1, 0, B), E8, R("t0f", p=8), True, True)
-    fill(R("k15"), 15.5)
-    mm(R(PQ, 0, B), R("idb"), R("mkb"), True, False)
-    mm(R(PQ, 0, B), R("nid"), R("k15"), False, False)
-    mm(R(PQ, 0, B), E8, R("t0f", p=8), False, True)
-    mm(R(PW, B, 2 * B), R("idb"), R("mkb"), True, False)
-    mm(R(PW, B, 2 * B), E8, R("l0f", p=8), False, True)
-    fill(R("av"), 1.0)
+    iota(R("ve", p=8), [[-1, 8], [0, 16]], 0, 1)
+    iota(R("vf", p=16), [[0, 8], [-1, 16]], 0, 1)
+    iota(R("ip"), [[0, 8]], 0, 1)
+    iota(R("i16"), [[16, 32]], 0, 0)
+    iota(R("vb"), [[-16, 8], [128, 2], [-2, 8]], 0, 1)
+    iota(R("va"), [[-16, 8], [0, 16]], 0, 1)
+    iota(R("vc"), [[-1, 128]], 0, 1)
+    fill(R("r3"), 2 * OFF)
     fill(R("r8"), 255.0)
-    fill(R("r8", 0, 8 * 44, 8), 0.0)
-    ts(R("pg"), R("ip"), 4, Op.arith_shift_right)
-    tt(R("gb"), R("pg"), R("mg"), Op.is_equal)
-    for nm, base in (("elo", 0), ("ehi", 16), ("olo", -1), ("ohi", 15)):
-        pick(R(nm), R("gb"), base, -2)
-    act(R("gs"), R("gb"), Act.Copy, scale=float(2 ** 16))
-    fill(R("rd"), 0.0)
-    fill(R("rd", 0, 784, 112), 4096.0)
-    fill(R("eq"), 4096.0)
-    ts(R("q16"), R("im", 0, 8), 16, Op.mult)
-    tt(R("iw"), R("q16"), R("p15", 0, 8), Op.add)
+    fill(R("da"), 1.0)
+    fill(R("db"), 0.0)
+    fill(R("r3", 0, B, 16), -2 * OFF)
+    fill(R("r8", 0, 8 * 32, 8), 0.0)
+    for k, v in ((0, 0.0), (1, 0.0), (3, -1.0), (6, -1.0)):
+        fill(R("da", k, 49, 7), v)
+    for k, v in ((0, 1.0), (4, 2.0), (5, 1.0), (6, -0.5)):
+        fill(R("db", k, 50, 7), v)
+    E8 = R("e8", p=8)
+    ts(E8, R("ve", p=8), 0.0, Op.is_equal)
+    ts(F16, R("vf", p=16), 0.0, Op.is_equal)
+    ts(FM, R("vf", 0, B, p=16), 0.0, Op.not_equal, -OFF, Op.mult)
+    ts(R("p15"), R("ip"), 15, Op.bitwise_and)
+    mm(R(BS, 0, 128), E8, E8, True, True)
+    fill(slot(4), M32)
+    cp(R("pf"), R("p15"))
+    fill(slot(5), -M32)
+    ts(R("idl"), R("i16"), R("pf", 0, 1), Op.add)
+    ts(R("iw"), R("i16", 0, 16), R("pf", 0, 1), Op.add)
+    ts(R("u5", p=8), R("tki", p=8), 31, Op.bitwise_and)
+    ts(R("l32", p=8), R("lni", p=8), 32.0, Op.mult)
+    cp(R("t5b", p=8), R("u5", p=8))
+    act(R("gb"), R(BS, 0, 128), Act.Copy)
+    act(R("gp"), R(BS, 0, 128), Act.Copy, scale=HI)
+    act(R("gn"), R(BS, 0, 128), Act.Copy, scale=-HI)
+    mm(R(BQ, 0, B), F16, FM, True, False)
+    mm(R(BQ, 0, B), E8, R("l32", p=8), False, False)
+    mm(R(BQ, 0, B), E8, R("t5b", p=8), False, True)
+    mm(R(BX, 0, B), E8, R("t5b", p=8), True, True)
+    ts(FM8, FM, 8.0, Op.add)
+    fill(R("pb", P0, P0 + 1), 0.0)
 
-    def lines_of(j):
-        a, b = j * C4, (j + 1) * C4
-        ts(R("lf", a, b), R("ili", a, b), -15.5, Op.add)
-
-    def lines_act(j):
-        a, b = j * C4, (j + 1) * C4
-        act(R("lg", a, b), R("lf", a, b), Act.Identity, MAGIC)
-        act(R("lt", a, b), R("lg", a, b), Act.Identity, -MAGIC)
+    def low_bits(j):
+        a, b = IL[j], IL[j + 1]
+        ts(R("an", a, b), R("ili", a, b), 31, Op.bitwise_and)
 
     def waits_of(j):
-        a, b = j * C4, (j + 1) * C4
-        bank = (PW, PL, PZ, PQ)[j]
-        mm(R(bank, 0, C4), R("idb"), R("lt", a, b), True, True)
-        tt(R("wt", a, b), R("ili", a, b), R(bank, 0, C4), Op.subtract)
+        a, b = IL[j], IL[j + 1]
+        act(R("wt", a, b), IND(R("an", a, b), R("idl", 0, (b - a) // 16)), Act.Copy)
 
-    SEG = lambda name, k=0: R(name, k * B + 15, (k + 1) * B, 16)
-    S7 = lambda name: R(name, 0, 7)
+    turn(R("km"), R(BQ, 0, B))
+    act(R("xr"), R(BX, 0, B), Act.Copy)
+    act(R("mo", 3 * B, 4 * B), R(BX, 0, B), Act.Identity, -6.5)
+    send(nxt, R("mi", 3 * B, 4 * B), R("mo", 3 * B, 4 * B), "ck")
+    low_bits(0)
+    cp(S7("o0"), SEG)
+    waits_of(0)
+    for nm, v in (("olo", 1.0), ("ohi", 129.0), ("elo", 0.0), ("ehi", 128.0)):
+        ts(R(nm), R("vb"), v, Op.is_equal)
+    low_bits(1)
+    waits_of(1)
+    ts(R("idb"), R("vc"), 0.0, Op.is_equal)
+    ts(R("nid"), R("vc"), 0.0, Op.is_equal, -1.0, Op.mult)
+    ts(R("se0"), R("va"), 0.0, Op.is_equal)
+    ts(R("se1"), R("va"), 1.0, Op.is_equal)
+    ts(R("s15"), R("va"), 15.0, Op.is_equal, 256.0, Op.mult)
+    tt(R("sd"), R("se1"), R("se0"), Op.subtract)
+    fill(R("neg"), -1.0)
+    fill(R("onb"), 1.0)
+    fill(R("da", 51, 52), -LO / 128)
+    fill(R("da", 58, 59), 9.0 / 128)
+    ts(slot(0, 1), S7("iw"), 16.0, Op.mult, LO, Op.add)
+    ts(S7("cwn"), S7("iw"), -1.0 / 4096, Op.mult, -W / 4096.0, Op.add)
+    fill(R("ob", B - 1, B), 0.0)
+    fill(R("am", 0, 1), 9.0 - 8200.0)
+    fill(R("dt"), 0.0)
+    low_bits(2)
+    waits_of(2)
+    fill(R("mo", 2 * B, 3 * B), LO)
+    fill(R("eq"), 4096.0)
+    fill(R("rd"), 0.0)
+    fill(R("rd", 0, 7 * B, B), 4096.0)
 
-    def parts_of(n):
-        m0, m1 = (0, 3) if n == 6 else (3, 4)
-        hi = n + 1
-        cp(R("si", 0, 8 * hi, p=B), R("sall", 0, 8 * hi, p=B))
-        ts(R("ai", 0, hi), R("av", 0, hi), -1.0, Op.add)
-        ts(R("sj", 0, 8 * hi, p=B), R("si", 0, 8 * hi, p=B), 31, Op.bitwise_and)
-        ts(R("aj", 0, hi), R("ai", 0, hi), 31, Op.bitwise_and)
-        tt(R("pp", 8 * m0, 8 * m1, p=B), R("sj", 8 * m0, 8 * m1, p=B), R("sj", 8 * m0 + 32, 8 * m1 + 32, p=B), Op.add)
-        tt(R("af", m0, m1), R("aj", m0, m1), R("aj", m0 + 4, m1 + 4), Op.add)
-        if n == 6:
-            fill(R("pt"), 0.0)
-        for j in range(m0, m1):
-            ts(R("pt", 8 * j, 8 * j + 8, p=B), R("pp", 8 * j, 8 * j + 8, p=B), R("af", j, j + 1, p=B), Op.add, 2.0, Op.add)
-            if j > 0:
-                send(cores[(rank - j) % NR], R("tpa", 8 * j, 8 * j + 8), R("pt", 8 * j, 8 * j + 8), "tp%d" % j)
-
-    def tail_of(n):
-        if n < 7:
-            act(R("af1"), R(P7, 256, 257), Act.Identity, MAGIC)
-            act(R("af2"), R("af1"), Act.Identity, MAGIC, scale=-1.0)
-            act(R("av", n + 1, n + 2), R(P7, 256, 257), Act.Identity, R("af2"))
-        if n >= 6:
-            parts_of(n)
-
-    for n in range(STEPS + 1):
-        last = n == STEPS
-        y0 = 224 * n
-        z, clk = R("yb", y0, y0 + B), R("yb", y0 + B, y0 + 2 * B)
-        lns, rot = (None, None) if last else (R("lr", y0, y0 + B), R("lr", y0 + B, y0 + 2 * B))
-        if n > 0:
-            k = n - 1
-            e0 = 224 * k
-            ey, ec = R("ey", e0, e0 + B), R("ey", e0 + B, e0 + 2 * B)
-            el, et = R("er", e0, e0 + B), R("er", e0 + B, e0 + 2 * B)
-            landed("ea%d" % k, prv, [("ey", e0, e0 + (224 if k < 7 else 112))])
-            landed("eb%d" % k, prv, [("er", e0, e0 + 224)])
-            KM = R(P6, 256, 256 + B)
-            mm(KM, R("s15"), el, False, False)
-            mm(KM, R("s15"), et, False, True)
-            mm(R(PK, 0, B), R("s15"), el, False, False)
-            mm(R(PK, 0, B), R("s15"), et, False, True)
-            if not last:
-                mm(R(P7, B, 2 * B), R("gb"), R("ge2"), True, True)
-            for c in (0, B):
-                mm(R(PW, c, c + B), R("idb"), R("mkb"), True, False)
-                if c:
-                    mm(R(PW, c, c + B), R("se1"), el, False, False)
-                mm(R(PW, c, c + B), R("nse" if c else "se0"), el, False, True)
-            mm(R(PZ, 0, B), R("nid"), ey, True, False)
-            if not last:
-                mm(R(PQ, 0, B), R("idb"), R("mkb"), True, False)
-                mm(R(PQ, 0, B), R("nid"), R("k15"), False, False)
-                mm(R(PQ, 0, B), R("idb"), ec, False, False)
-                mm(R(P1, 0, B), R("idb"), ec, True, False)
-                UC = R(P7, 280, 280 + B)
-                PX, PE, PO, PR = R(PW, 256, 256 + B), R(PL, 0, 56), R(PZ, 128, 184), R(P6, 128, 128 + B)
-            scan(R("w3", 0, B), R("r3", 0, B), KM, 0.0, Op.min, Op.max)
-            tt(S7("nb"), S7("c1"), SEG("w3"), Op.subtract)
-            for q in range(7):
-                L = 16 * q + 16
-                act(R("eq", 112 * q + 112 - L, 112 * q + 112), R(PK, 0, L), Act.Abs, R("nb", q, q + 1))
-            ts(S7("dof0"), S7("nb"), -1.0 / 256, Op.mult)
-            ts(S7("nk"), S7("nb"), 2.0 ** -20, Op.mult)
-            ts(R("wdm"), IND(R("wt"), S7("dof0")), -32.0, Op.add)
-            tt(S7("nk"), S7("nk"), S7("iw"), Op.subtract)
-            scan(R("em", 0, 448), R("rd", 0, 448), R("eq", 0, 448), 4096.0, Op.max, Op.min)
-            scan(R("em", 448, 784), R("rd", 448, 784), R("eq", 448, 784), 4096.0, Op.max, Op.min)
-            scan(R("w3", B, 3 * B), R("r3", B, 3 * B), R(PW, 0, 2 * B), 0.0, Op.min, Op.max)
-            tt(S7("tp8"), R("em", 111, 784, 112), S7("nk"), Op.add)
-            ts(S7("dl"), SEG("w3", 2), -BIG, Op.add)
-            ts(S7("lbx"), SEG("w3", 1), -BIG, Op.add)
-            tt(S7("mn"), S7("tp8"), S7("cwn"), Op.max)
-            ts(S7("doff"), S7("mn"), -4096.0, Op.mult)
-            if last:
-                mm(R(P6, 0, B), R("se0"), el, True, True)
-                mm(R(P6, B, 2 * B), R("se1"), el, True, False)
-                mm(R(P6, B, 2 * B), R("nse"), el, False, True)
-            if not last:
-                act(R("jk"), R(P7, B, 2 * B), Act.Sign, -1.0, R("acc"))
-                mm(R(P7, 256, 257), R("on32"), R("q25"), True, False)
-                mm(R(P7, 256, 257), R("on32"), R("acc"), False, True)
-                if n == 7:
-                    tail_of(k)
-            landed("zr%d" % k, prv, z[1])
-            mm(R(PZ, 0, B), R("idb"), z, False, True)
-            if not last:
-                mm(R(PQ, 0, B), R("gb"), z, False, False)
-                mm(R(P1, 0, B), R("gb"), z, False, True)
-                tt(IND(R("wt"), S7("doff")), R("wdm"), z, Op.add)
-            act(R("ge"), R(PZ, 0, B), Act.Sign, 0.5)
-            mm(R(PQ, 0, B), R("gb" if last else "gs"), R("ge"), last, True)
-            if not last:
-                mm(UC, R("idb"), ec, True, False)
-                mm(UC, R("gb"), z, False, False)
-                mm(PX, R("idb"), R("k15"), True, False)
-        if last:
-            break
-        scan(R("qw"), R("r3", 0, B), R(PQ, 0, B), 0.0, Op.min, Op.max)
-        if n == 0:
-            scan(R("w3", B, 2 * B), R("r3", B, 2 * B), R(PW, B, 2 * B), 0.0, Op.min, Op.max)
-            ts(S7("lbx"), SEG("w3", 1), -BIG, Op.add)
-        tt(S7("ta"), SEG("qw"), S7("lbx"), Op.add)
-        if n > 0:
-            ts(S7("sk"), SEG("qw"), BIG + 2.0 ** 16, Op.is_ge)
-        ts(S7("mn"), SEG("qw"), MAGIC, Op.add, -MAGIC, Op.add)
-        if n > 0:
-            ts(S7("qi"), SEG("qw"), 15.5, Op.add)
-            tt(S7("sd"), S7("sk"), S7("dl"), Op.mult)
-        tt(S7("ta"), S7("ta"), S7("mn"), Op.subtract)
-        if n > 0:
-            ts(S7("tq"), S7("qi"), 15, Op.bitwise_and)
-            tt(S7("ta"), S7("ta"), S7("sd"), Op.add)
-            tt(R("ta", 8, 15), S7("tq"), R("lbx", 8, 15), Op.add)
-        ts(S7("offs"), S7("ta"), 15.5, Op.add)
-        if n > 0:
-            cp(R("offs", 8, 15), R("ta", 8, 15))
-        act(R("uf"), R(P1, 0, B), Act.Identity, MAGIC)
-        act(R("ug"), R("uf"), Act.Identity, -MAGIC)
-        if n == 0:
-            UC = R(P7, 280, 280 + B)
-            mm(UC, E8, R("t0f", p=8), True, False)
-        mm(UC, R("nid"), R("ug"), False, True)
-        if n > 0:
-            act(R("xr"), UC, Act.Copy)
-        if n > 0:
-            act(R("wf"), IND(R("wt"), S7("offs")), Act.Copy)
-            act(lns, IND(R("lt"), S7("offs")), Act.Copy)
-            if n < 7:
-                tail_of(n - 1)
-        if n < 7:
-            act(clk, UC, Act.Identity, R("av", n, n + 1))
-        if n > 0:
-            cp(IND(R("xt"), R("offs", 8, 15)), z)
-            lists = ((PO, "olo", "ohi"), (PE, "elo", "ehi"))
-
-            def halves(pb, lo, hi, name, a, start, stop):
-                mm(pb, R(lo), R(name, a, a + B, 2), start, False)
-                mm(pb, R(hi), R(name, a + 1, a + B, 2), False, stop)
-            for pb, lo, hi in lists:
-                halves(pb, lo, hi, "xr", 0, True, False)
-            mm(PR, R("idb"), R("xr"), True, False)
-            mm(PX, R("nid"), R("xr"), False, False)
-            mm(PX, R("nid"), R("wf"), False, True)
-            ts(R("flx"), PX, MAGIC, Op.add, -MAGIC, Op.add)
-            halves(PO, "olo", "ohi", "wf", 0, False, False)
-            halves(PO, "olo", "ohi", "lr", y0, False, False)
-            halves(PO, "olo", "ohi", "flx", 0, False, True)
-            mm(PR, R("idb"), R("wf"), False, False)
-            mm(PR, R("idb"), R("flx"), False, True)
-            halves(PE, "elo", "ehi", "wf", 0, False, False)
-            halves(PE, "elo", "ehi", "lr", y0, False, False)
-            halves(PE, "elo", "ehi", "flx", 0, False, True)
-            tt(R("rz"), R("wdm"), z, Op.add)
-            cp(R("sod"), PO)
-            ts(R("ry"), R("rz"), 31, Op.bitwise_and)
-            cp(R("sev"), PE)
+    def gains(n, k):
+        SZ, zall, G8 = R(BS, 0, 8, p=B), R("zo", B * n, B * n + B), R("gb", 0, 128, 16)
+        if k == 0:
+            mm(SZ, zall, G8, True, True)
+        elif k == 1:
+            act(R("fz", p=B), SZ, Act.Identity, 8192.0 + 15.5, scale=-1.0)
+            if n < STEPS - 1:
+                act(R("am", n + 1, n + 2), R("av", n + 1, n + 2), Act.Identity, -8200.0)
         else:
-            fill(R("wt", W, WT), 0.0)
-            fill(R("q25"), 0.25)
-            fill(R("on32"), 1.0 / 32)
-            cp(R("iob"), R("im", 0, B))
-            tt(R("g8"), R("pg", 0, 8), R("im", 0, 8), Op.is_equal)
-            ts(S7("c1"), S7("iw"), BIG, Op.add)
-            ts(S7("cwn"), S7("iw"), -1.0 / 4096, Op.mult, -W / 4096.0, Op.add)
-            ts(R("lbx", 8, 15), S7("iw"), 16.0, Op.mult)
-            for j in range(3):
-                lines_of(j)
-                lines_act(j)
-            cp(R("ci"), IND(R("ili"), S7("offs")))
-            tt(R("ui"), R("ci"), R(P1, 0, B), Op.add)
-            ts(R("cl"), R("ci"), 4064, Op.bitwise_and)
+            mm(SZ, zall, G8, True, False)
+            mm(SZ, (T.idb[0:B, 0:B], R("idb")[1], []), R("fz", p=B), False, True)
+            d0 = 16 * (n % 4) + 8 * (n // 4)
+            act(R("dt", d0, d0 + 8, p=B), SZ, Act.Identity, R("am", n, n + 1, p=B))
+
+    def gains_home(j):
+        e = 16 * j + 16 if j < 3 else 64 + B
+        send(cores[(rank - j) % NR], R("di", 16 * j, e), R("dt", 16 * j, e), "tp%d" % j)
+
+    for n in range(STEPS):
+        last = n == STEPS - 1
+        y, zo, z = R("zi", B * n, B * n + B), B * n, R("zi", B * n + B, B * n + 2 * B)
+        m0 = 4 * B * n
+        part = lambda name, k: R(name, m0 + k * B, m0 + k * B + B)
+        fetch = S7("o0") if n == 0 else R("oi", 16 * n - 16, 16 * n - 9)
+        if n == 0:
+            tt(R("ui"), IND(R("ili"), fetch), R("xr"), Op.add)
+            act(part("mo", 0), IND(R("ili"), fetch), Act.Identity, LO - 15.5)
             ts(R("u5"), R("ui"), 31, Op.bitwise_and)
-            cp(lns, R("cl"))
-            cp(rot, R("u5"))
-            for pb, lo, hi, od in ((R(PZ, 128, 184), "olo", "ohi", "sod"), (R(PL, 0, 56), "elo", "ehi", "sev")):
-                for o in (0, B):
-                    mm(pb, R(lo), R("lr", o, o + B, 2), o == 0, False)
-                    mm(pb, R(hi), R("lr", o + 1, o + B, 2), False, o > 0)
-                cp(R(od), pb)
-            lines_of(3)
-            waits_of(0)
+            low_bits(3)
+            ts(part("mo", 1), R("u5"), -15.5, Op.add)
+            waits_of(3)
+        else:
+            landed("of%d" % (n - 1), prv, R("oi", 16 * n - 16, 16 * n))
+            tt(part("mo", 1), IND(R("wt", 0, W), fetch), R("xr"), Op.add)
+            act(part("mo", 0), IND(R("ili"), fetch), Act.Identity, LO - 15.5)
+            ts(part("mo", 2), part("mo", 1), -1.0, Op.mult, LO, Op.add)
+            cp(IND(R("xt"), R("oi", 16 * n - 8, 16 * n - 1)), y)
+            if not last:
+                act(part("mo", 3), R("xr"), Act.Identity, R("av", n, n + 1))
+        mw = 4 * B if 0 < n < STEPS - 1 else 3 * B
+        send(nxt, R("mi", m0, m0 + mw), R("mo", m0, m0 + mw), "ea%d" % n)
+        act(R(BL, 0, B), y, Act.Relu, -1.0, scale=2.0)
         if n > 0:
-            act(rot, PR, Act.Copy)
+            gains(n - 1, 1)
+        terms = (1, 0, 2) if n > 0 else (0, 1)
+        for pb, lo, hi, od in ((R(BO, 0, 56), "olo", "ohi", "sod"), (R(BE, 0, 56), "elo", "ehi", "sev")):
+            for k in terms:
+                a = m0 + k * B
+                mm(pb, R(lo), R("mo", a, a + B, 2), k == terms[0], False)
+                mm(pb, R(hi), R("mo", a + 1, a + B, 2), False, k == terms[-1])
+            ts(R(od), pb, -C0 if n > 0 else LO - C0, Op.add)
         for a, b in zip(CH, CH[1:]):
             act(R("vo", 8 * a, 8 * b), IND(R("xt"), R("sod", a // 2, b // 2)), Act.Copy)
-            if a == 0:
-                send(nxt, R("er", y0, y0 + 224), R("lr", y0, y0 + 224), "eb%d" % n)
-                ew = 224 if n < 7 else 112
-                send(nxt, R("ey", y0, y0 + ew), R("yb", y0, y0 + ew), "ea%d" % n)
-        M = CH[-3]
-        mm(R(PK, 0, M), R("nid"), R("yb", y0, y0 + M), True, False)
-        mm(R(P6, 0, B - M), R("nid"), R("yb", y0 + M, y0 + B), True, False)
-
-        def least(k):
-            a, b = CH[k], CH[k + 1]
-            tt(R("mn2", 8 * a, 8 * b), IND(R("xt"), R("sev", a // 2, b // 2)), R("vo", 8 * a, 8 * b), Op.min)
-
-        def greatest(a, b):
-            scan(R("mx", 8 * a, 8 * b), R("r8", 0, 8 * (b - a)), R("mn2", 8 * a, 8 * b), 0.0, Op.min, Op.max)
-        for k in range(len(CH) - 1):
-            least(k)
-            if k > 0:
-                greatest(CH[k - 1], CH[k])
-        greatest(CH[-2], B)
-        zo = B * n
-        mm(R(PK, 0, M), R("idb"), R("mx", 7, 8 * M, 8), False, True)
-        mm(R(P6, 0, B - M), R("idb"), R("mx", 8 * M + 7, 8 * B, 8), False, True)
-        act(R("zo", zo, zo + M), R(PK, 0, M), Act.Abs)
-        act(R("zo", zo + M, zo + B), R(P6, 0, B - M), Act.Abs)
-        zo = R("zo", zo, zo + B)
-        send(nxt, R("yb", y0 + 224, y0 + 224 + B), zo, "zr%d" % n)
+        DL, L0, Q, KM, PK = R(BL, B, 2 * B), R(BL, 2 * B, 3 * B), R(BQ, 0, B), R(BK, 0, B), R(BP, 0, B)
+        DE, DZ = R(BO, 128, 128 + EARLY), R(BE, 128, 128 + B - EARLY)
         if n > 0:
-            cp(IND(R("wt"), S7("doff")), R("ry"))
-        KM = R(P6, 256, 256 + B)
-        mm(KM, R("idb"), R("mkb"), True, False)
-        mm(KM, R("idb"), R("iob"), False, False)
-        mm(R(PK, 0, B), R("idb"), R("iob"), True, False)
-        if n == 0:
-            lines_act(3)
-            for j in range(1, 4):
-                waits_of(j)
-        if n < 7:
-            mm(R(P7, 0, B), R("nid"), z, True, False)
-            mm(R(P7, 0, B), R("idb"), zo, False, True)
-            act(R("ge2"), R(P7, 0, B), Act.Sign, 0.5)
-        mm(R(PL, 264, 272, p=B), zo, R("g8"), True, True)
-        act(R("sall", 8 * n, 8 * n + 8, p=B), R(PL, 264, 272, p=B), Act.Copy)
-        if n == 7:
-            tail_of(n)
+            gains(n - 1, 2)
+            if n > 5:
+                gains_home(n - 5)
+        if not last:
+            mm(DL, F16, FM, True, False)
+        mm(DL, R("sd"), part("mo", 0), last, True)
+        if not last:
+            mm(L0, F16, FM8, True, False)
+        mm(L0, R("se0"), part("mo", 0), last, True)
+        mm(DE, R("nid"), R("zi", B * n, B * n + EARLY), True, False)
+        mm(DZ, R("nid"), R("zi", B * n + EARLY, B * n + B), True, False)
+        if not last:
+            mm(Q, F16, FM, True, False)
+            mm(Q, R("idb"), part("mo", 3), False, False)
+        mm(KM, F16, FM, True, False)
+        landed("ea%d" % n, prv, R("mi", m0, m0 + mw))
+        for k in range(3):
+            mm(KM, R("s15"), part("mi", k), False, k == 2)
+        done = [0]
 
-    tt(R("rz"), R("wdm"), z, Op.add)
-    ts(R("ry"), R("rz"), 31, Op.bitwise_and)
-    cp(IND(R("wt"), S7("doff")), R("ry"))
-    dma("Y", T.yw[:, :], T.wt[:, 0:W], [("wt", 0, W)], [])
-    dma("S", T.yy[:, :], T.yb[:, y0:y0 + B], z[1], [])
-    ts(R("fs"), R(PQ, 0, B), 1.0, Op.is_ge)
-    tt(R("fd"), R("fs"), R(P6, B, 2 * B), Op.mult)
-    tt(R("fl"), R("fd"), R(P6, 0, B), Op.add)
-    ts(R("fy"), R("fl"), 1.0 / 32, Op.mult)
-    dma("S", T.yl[:, :], T.fy[0:128:16, :], [("fy", 0, B)], [])
-    for j in range(1, 4):
-        landed("tp%d" % j, cores[(rank + j) % NR], [("tpa", 8 * j, 8 * j + 8)])
-    idq = (T.idf[0:B, 0:B], [("idf", 0, B)], [])
+        def greatest(upto):
+            while done[0] < len(SC) - 1 and SC[done[0] + 1] <= upto:
+                a, b = SC[done[0]], SC[done[0] + 1]
+                scan(R("mx", 8 * a, 8 * b), R("r8", 0, 8 * (b - a)), R("mn2", 8 * a, 8 * b), 0.0, Op.min, Op.max)
+                done[0] += 1
+        for a, b in zip(CH, CH[1:]):
+            tt(R("mn2", 8 * a, 8 * b), IND(R("xt"), R("sev", a // 2, b // 2)), R("vo", 8 * a, 8 * b), Op.min)
+            greatest(a)
+        greatest(B)
+        for a, b, D in ((0, EARLY, DE), (EARLY, B, DZ)):
+            m = R("mx", 8 * a + 7, 8 * b, 8)
+            mm(D, R("idb"), m, False, True)
+            act(R("sg", a, b), m, Act.Sign)
+            act(R("zo", zo + a, zo + b), D, Act.Abs)
+            if a == 0:
+                mm(R(BQ, a, b), R("gn"), R("sg", a, b), last, False)
+                if not last:
+                    mm(R(BQ, a, b), R("gb"), R("zo", zo + a, zo + b), False, False)
+        send(nxt, z, R("zo", zo, zo + B), "zr%d" % n)
+        if not last:
+            turn(into(1), DL)
+        tt(R("ge"), R("mx", 7, 8 * B, 8), R(BL, 0, B), Op.is_gt)
+        if last:
+            mm(R(BQ, 0, EARLY), R("gp"), R("ge", 0, EARLY), False, True)
+            mm(R(BQ, EARLY, B), R("gn"), R("sg", EARLY, B), True, False)
+            mm(R(BQ, EARLY, B), R("gp"), R("ge", EARLY, B), False, True)
+        else:
+            mm(R(BQ, EARLY, B), R("gn"), R("sg", EARLY, B), False, False)
+            mm(Q, R("gp"), R("ge"), False, False)
+            mm(R(BQ, EARLY, B), R("gb"), R("zo", zo + EARLY, zo + B), False, True)
+            turn(into(2), L0)
+        turn(R("km"), KM)
+        mm(PK, R("neg", p=1), R("vc", 0, B, p=1), True, False)
+        for k in range(3):
+            mm(PK, R("s15"), part("mi", k), False, k == 2)
+        ts(S7("dof0"), SEG, 1.0 / 256, Op.mult, -C0, Op.add)
+        for q in range(7):
+            L = 16 * q + 16
+            act(R("eq", B * q + B - L, B * q + B), R(BP, 0, L), Act.Abs, R("km", 16 * q + 15, 16 * q + 16), scale=-1.0)
+        thr = -7 * HI - 64
+        if not last:
+            turn(into(6), Q)
+            ts(S7("nk"), SEG, -2.0 ** -20, Op.mult, C0 / 4096, Op.add)
+            ts(R("da", 2, 49, 7), slot(6), thr, Op.is_ge)
+            ts(slot(3), slot(6), M16, Op.add, -M16, Op.add)
+            tt(S7("nk"), S7("nk"), S7("iw"), Op.subtract)
+            scan(R("ob", 0, 49), R("da", 0, 49), R("pb", P0, P0 + 16 * 48 + 1, 16), 0.0, Op.mult, Op.add)
+            scan(R("ob", 55, 105), R("db", 0, 50), R("pb", P0, P0 + 16 * 49 + 1, 16), 0.0, Op.mult, Op.add)
+            ts(R("oo", 16 * n, 16 * n + 16), R("ob", 6, B, 7), 7.5 - LO, Op.add)
+            send(nxt, R("oi", 16 * n, 16 * n + 16), R("oo", 16 * n, 16 * n + 16), "of%d" % n)
+            mm(R(BQ, 128, 137), R("onb"), R("da", 2, 59, 7), True, True)
+        else:
+            ts(R("fs"), Q, thr, Op.is_ge)
+            ts(S7("nk"), SEG, -2.0 ** -20, Op.mult, C0 / 4096, Op.add)
+            tt(R("fd"), R("fs"), DL, Op.mult)
+            tt(S7("nk"), S7("nk"), S7("iw"), Op.subtract)
+            tt(R("fl"), R("fd"), L0, Op.add)
+        gains(n, 0)
+        act(R("wdb"), IND(R("wt", 0, W), S7("dof0")), Act.Copy)
+        mm(R(BK, 128, 128 + B), R("idb"), R("wdb"), True, True)
+        if not last:
+            act(R("jk", 0, 9), R(BQ, 128, 137), Act.Copy, acc=R("ac", 0, 1))
+            act(R("fa", 0, 1), R("ac", 0, 1), Act.Identity, 24.5, scale=-1.0)
+            act(R("av", n + 1, n + 2), R("ac", 0, 1), Act.Identity, R("fa", 0, 1))
+        else:
+            gains(n, 1)
+            gains(n, 2)
+        scan(R("em", 0, 448), R("rd", 0, 448), R("eq", 0, 448), 4096.0, Op.max, Op.min)
+        if last:
+            ts(R("dt", 64, 64 + B), R("fl"), 1.0 / 32, Op.mult, -LO / 32, Op.add)
+        scan(R("em", 448, 784), R("rd", 448, 784), R("eq", 448, 784), 4096.0, Op.max, Op.min)
+        if last:
+            gains_home(3)
+        X1, X2 = R(BP, 128, 128 + B), R(BX, 0, B)
+        if not last:
+            if n == 0:
+                landed("ck", prv, part("mi", 3))
+            mm(X1, R("idb"), part("mi", 3), True, False)
+            mm(X2, R("idb"), part("mi", 3), True, False)
+        tt(S7("tp8"), R("em", B - 1, 7 * B, B), S7("nk"), Op.add)
+        landed("zr%d" % n, prv, z)
+        tt(S7("mn"), S7("tp8"), S7("cwn"), Op.max)
+        tt(R("rz"), z, R(BK, 128, 128 + B), Op.add)
+        ts(S7("doff"), S7("mn"), -4096.0, Op.mult)
+        ts(R("ry"), R("rz"), 31, Op.bitwise_and)
+        cp(IND(R("wt"), S7("doff")), R("ry"))
+        if not last:
+            mm(X1, R("gb"), z, False, True)
+            mm(X2, R("gb"), z, False, False)
+            act(R("fx"), X1, Act.Identity, 14336.0, scale=-1.0)
+            mm(X2, R("idb"), R("fx"), False, True)
+            act(R("xr"), X2, Act.Identity, -14344.0)
+
+    dma("Y", T.yw[:, :], T.wt[:, 0:W], R("wt", 0, W)[1], [])
+    dma("S", T.yy[:, :], T.zi[:, 8 * B:9 * B], z[1], [])
+    idq = (T.idb[0:B, 0:B], R("idb")[1], [])
     for j in range(4):
-        mm(R(P1, 0, B, p=8), R("pt" if j == 0 else "tpa", 8 * j, 8 * j + 8, p=B), idq, j == 0, j == 3)
-    tt(R("ft", p=8), R("tki", p=8), R(P1, 0, B, p=8), Op.add)
+        if j > 0:
+            landed("tp%d" % j, cores[(rank + j) % NR], R("di", 16 * j, 16 * j + 16 if j < 3 else 64 + B))
+        for h in range(2):
+            a = 16 * j + 8 * h
+            mm(R(BQ, 0, B, p=8), R("dt" if j == 0 else "di", a, a + 8, p=B), idq, a == 0, a == 56)
+    act(R("fy"), R("di", 64, 64 + B), Act.Copy)
+    dma("S", T.yl[:, :], T.fy[0:128:16, :], R("fy")[1], [])
+    tt(R("ft", p=8), R("tki", p=8), R(BQ, 0, B, p=8), Op.add)
     ts(R("fu", p=8), R("ft", p=8), 4095, Op.bitwise_and)
     cp(R("fv", p=8), R("fu", p=8))
-    dma("Y", T.yt[:, :], T.fv[0:8, :], [("fv", 0, B)], [])
+    dma("Y", T.yt[:, :], T.fv[0:8, :], R("fv")[1], [])
     for q in ("V", "S", "P", "G"):
         g.wait_ge(T.sem[sems[q]], cnt[q])
     for name in dma_all:

@@ -6,34 +6,43 @@ M16, M32 = float(3 * 2 ** 26), float(3 * 2 ** 27)
 LO = 6144.0
 C0 = 2 * LO - 15.5
 HI = 8192.0
-CH = (0, 8, 28, 56, 88, B)
-SC = (0, 28, 56, 88, B)
+CH = (0, 12, 32, 56, 84, B)
+SC = (0, 32, 56, 84, B)
 EARLY = 56
+PKE, WDE, LOW, CK, KL = (2, 0), 2, "aacd", 1, 1
+SKQ = 5
+RZE = (0, 0)
+UP, TOP, ES = float(2 ** 30), float(2 ** 22), float(2 ** 14)
+THR = -7 * HI - 64
+LD = (0, 960, W)
 IL = (0, 480, 960, 1440, W)
-WT = W + B
+DUMP = 2048
+WT = DUMP + 16 * B
 P0 = 89
+EQ = (0, 56, 112, 168, 280, 392, 504, 616)
+E0 = 550
 
 SCRATCH = {}
 for _names, _w, _t in (
         ("xt", W, "bfloat16"), ("wt", WT, "bfloat16"), ("ili an", W, "int32"),
         ("tki lni ui u5 rz ry ft fu", B, "int32"), ("ip", 8, "int32"), ("p15", 8, "int32"),
-        ("km fy fv", B, "float32"), ("pf ac", 8, "float32"), ("i16", 32, "float32"),
-        ("t5b l32 fm fm8 xr wdb ge sg fx r3 fs fd fl", B, "bfloat16"),
-        ("va vb vc ve e8 vf onb neg f16 idb nid gb gp gn se0 se1 sd s15 elo ehi olo ohi", 128, "bfloat16"),
-        ("iw cwn nk tp8 mn av am jk", 16, "float32"), ("fa fz", 8, "bfloat16"),
+        ("km fy fv", B, "float32"), ("pf ac sc up kb", 8, "float32"), ("ka kc kk", B, "bfloat16"), ("i16", 32, "float32"), ("dx xo", 40, "float32"),
+        ("t5b l32 xr wdb sy s0 s1 wn r3 fs fd fl", B, "bfloat16"), ("fm fx", 2 * B, "bfloat16"),
+        ("va vb vc ve e8 vf onb neg f16 idb nid n2d gb g2 gp gn se0 se1 sd s15 elo ehi olo ohi", 128, "bfloat16"),
+        ("iw dd mn av am jk", 16, "float32"), ("fa fz", 8, "bfloat16"),
         ("doff dof0", 8, "uint16"), ("o0", 16, "uint16"), ("idl", 32, "uint16"), ("sev sod", 56, "uint16"),
-        ("rd eq em", 7 * B, "bfloat16"), ("r8", 8 * 32, "bfloat16"), ("vo mn2 mx", 8 * B, "bfloat16"),
-        ("pb", 880, "float32"), ("da db", 64, "bfloat16"), ("ob", B, "float32"),
+        ("rd eq", EQ[7], "bfloat16"), ("em", 38 * B, "bfloat16"), ("r8", 8 * 32, "bfloat16"), ("vo mn2 mx", 8 * B, "bfloat16"),
+        ("pb", 880, "float32"), ("da db", 64, "bfloat16"), ("ob", 808, "float32"),
         ("zi", 9 * B, "bfloat16"), ("zo", 8 * B, "bfloat16"),
         ("mo mi", 8 * 4 * B, "bfloat16"),
-        ("oo oi", 8 * 16, "uint16"),
+        ("oo", 8 * 24, "uint16"), ("oi", 8 * 16, "uint16"),
         ("dt di", 64 + B, "bfloat16")):
     for _n in _names.split():
         SCRATCH[_n] = ("sbuf", [128, _w], _t)
 PSUM = ["b%d" % i for i in range(8)]
 for _n in PSUM:
     SCRATCH[_n] = ("psum", [128, 512], "float32")
-SEMAPHORES = (["sV", "sS", "sP", "sG", "lsem", "ck", "tp1", "tp2", "tp3"] + ["%s%d" % (a, i) for a in ("zr", "ea", "of") for i in range(8)]
+SEMAPHORES = (["sV", "sS", "sP", "sG", "lsem", "tp1", "tp2", "tp3"] + ["%s%d" % (a, i) for a in ("ck", "zr", "ea", "of") for i in range(8)]
               + ["d%d" % i for i in range(16)])
 
 
@@ -128,12 +137,12 @@ def rank_program(g, core, T, topo):
     def act(out, a, f, bias=None, acc=None, scale=None):
         kw = {}
         if scale is not None:
-            kw["scale"] = scale
+            kw["scale"] = ap(scale)
         if bias is not None:
             kw["bias"] = ap(bias)
         if acc is not None:
             kw["accum_out"] = acc[0]
-        emit("S", rd(a, bias), out[1] + (acc[1] if acc is not None else []),
+        emit("S", rd(a, bias, scale), out[1] + (acc[1] if acc is not None else []),
              lambda: S.activation(out=out[0], in_=a[0], func=f, **kw))
 
     def mm(out, l, r, start, stop):
@@ -169,20 +178,21 @@ def rank_program(g, core, T, topo):
     def landed(sem, src, reg):
         note(sem, len(topo.engines(src, core)), [], reg[1])
 
-    BQ, BL, BK, BP, BO, BE, BX, BS = PSUM
+    BQ, BL, BK, BP, BO, BE, BA, BB = PSUM
     S7 = lambda name: R(name, 0, 7)
     SEG = R("km", 15, B, 16)
     slot = lambda k, q0=0: R("pb", P0 + 16 * k + B * q0, P0 + 16 * k + B * (q0 + 6) + 1, B)
     into = lambda k: R("pb", P0 + 16 * k - 105, P0 + 16 * k - 105 + 7 * B, 7)
-    F16, FM, FM8 = R("f16", p=16), R("fm", p=16), R("fm8", p=16)
+    F16, FM = R("f16", p=16), R("fm", 0, B, p=16)
+    DL, L0, Q, KM = R(BL, 0, B), R(BL, B, 2 * B), R(BQ, 0, B), R(BK, 0, B)
+    sc = lambda k: R("sc", k, k + 1)
 
     def turn(out, src):
         scan(out, R("r3"), src, 0.0, Op.min, Op.max)
 
     dma("Y", T.tki[0:8, :], T.tk0[:, :], [], R("tki")[1])
     dma("S", T.lni[0:8, :], T.ln0[:, :], [], R("lni")[1])
-    for j in range(4):
-        a, b = IL[j], IL[j + 1]
+    for a, b in zip(LD, LD[1:]):
         dma("Y", T.ili[:, a:b], T.il[:, a:b], [], R("ili", a, b)[1])
     dma("Y", T.xt[:, :], T.xw[:, :], [], R("xt")[1])
     dma("Y", T.zi[:, 0:B], T.y0[:, :], [], R("zi", 0, B)[1])
@@ -194,39 +204,51 @@ def rank_program(g, core, T, topo):
     iota(R("vb"), [[-16, 8], [128, 2], [-2, 8]], 0, 1)
     iota(R("va"), [[-16, 8], [0, 16]], 0, 1)
     iota(R("vc"), [[-1, 128]], 0, 1)
+    iota(R("dt"), [[0, 64 + B]], 0, 0)
+    iota(R("mo", 2 * B, 3 * B), [[0, B]], int(LO), 0)
+
+    def put(out, v):
+        act(out, R("onb", 0, out[0].shape[1]), Act.Identity, v, scale=0.0)
+    fill(R("onb"), 0.5)
     fill(R("r3"), 2 * OFF)
     fill(R("r8"), 255.0)
-    fill(R("da"), 1.0)
-    fill(R("db"), 0.0)
+    fill(R("neg"), -1.0)
     fill(R("r3", 0, B, 16), -2 * OFF)
     fill(R("r8", 0, 8 * 32, 8), 0.0)
+    put(R("da"), 1.0)
+    put(R("db"), 0.0)
+    put(R("dx"), TOP)
+    put(R("em", E0 - B, E0 + 33 * B + 1, B), 0.0)
     for k, v in ((0, 0.0), (1, 0.0), (3, -1.0), (6, -1.0)):
-        fill(R("da", k, 49, 7), v)
+        put(R("da", k, 49, 7), v)
     for k, v in ((0, 1.0), (4, 2.0), (5, 1.0), (6, -0.5)):
-        fill(R("db", k, 50, 7), v)
+        put(R("db", k, 50, 7), v)
     E8 = R("e8", p=8)
     ts(E8, R("ve", p=8), 0.0, Op.is_equal)
     ts(F16, R("vf", p=16), 0.0, Op.is_equal)
     ts(FM, R("vf", 0, B, p=16), 0.0, Op.not_equal, -OFF, Op.mult)
     ts(R("p15"), R("ip"), 15, Op.bitwise_and)
-    mm(R(BS, 0, 128), E8, E8, True, True)
-    fill(slot(4), M32)
+    mm(R(BB, 0, 128), E8, E8, True, True)
+    ts(R("ka", p=16), R("vf", 0, B, p=16), 0.0, Op.not_equal)
     cp(R("pf"), R("p15"))
-    fill(slot(5), -M32)
+    ts(R("kc", p=16), R("vf", 0, B, p=16), -1.0, Op.is_equal, UP, Op.mult)
     ts(R("idl"), R("i16"), R("pf", 0, 1), Op.add)
     ts(R("iw"), R("i16", 0, 16), R("pf", 0, 1), Op.add)
+    ts(sc(2), R("pf", 0, 1), 15.0, Op.is_equal, 1.0 / UP, Op.max)
     ts(R("u5", p=8), R("tki", p=8), 31, Op.bitwise_and)
     ts(R("l32", p=8), R("lni", p=8), 32.0, Op.mult)
     cp(R("t5b", p=8), R("u5", p=8))
-    act(R("gb"), R(BS, 0, 128), Act.Copy)
-    act(R("gp"), R(BS, 0, 128), Act.Copy, scale=HI)
-    act(R("gn"), R(BS, 0, 128), Act.Copy, scale=-HI)
-    mm(R(BQ, 0, B), F16, FM, True, False)
-    mm(R(BQ, 0, B), E8, R("l32", p=8), False, False)
-    mm(R(BQ, 0, B), E8, R("t5b", p=8), False, True)
-    mm(R(BX, 0, B), E8, R("t5b", p=8), True, True)
-    ts(FM8, FM, 8.0, Op.add)
-    fill(R("pb", P0, P0 + 1), 0.0)
+    for nm, v in (("gb", 1.0), ("gp", HI / 2), ("g2", HI), ("gn", -HI / 2)):
+        act(R(nm), R(BB, 0, 128), Act.Copy, scale=v)
+    mm(R(BP, 0, B), F16, R("ka", p=16), True, False)
+    mm(R(BP, 0, B), F16, R("kc", p=16), False, True)
+    mm(Q, F16, FM, True, False)
+    mm(Q, E8, R("l32", p=8), False, False)
+    mm(Q, E8, R("t5b", p=8), False, True)
+    mm(R(BA, 0, B), E8, R("t5b", p=8), True, True)
+    act(R("kk"), R(BP, 0, B), Act.Copy)
+    for nm, v in (("olo", 1.0), ("ohi", 129.0), ("elo", 0.0), ("ehi", 128.0)):
+        ts(R(nm), R("vb"), v, Op.is_equal)
 
     def low_bits(j):
         a, b = IL[j], IL[j + 1]
@@ -236,41 +258,42 @@ def rank_program(g, core, T, topo):
         a, b = IL[j], IL[j + 1]
         act(R("wt", a, b), IND(R("an", a, b), R("idl", 0, (b - a) // 16)), Act.Copy)
 
-    turn(R("km"), R(BQ, 0, B))
-    act(R("xr"), R(BX, 0, B), Act.Copy)
-    act(R("mo", 3 * B, 4 * B), R(BX, 0, B), Act.Identity, -6.5)
-    send(nxt, R("mi", 3 * B, 4 * B), R("mo", 3 * B, 4 * B), "ck")
-    low_bits(0)
-    cp(S7("o0"), SEG)
-    waits_of(0)
-    for nm, v in (("olo", 1.0), ("ohi", 129.0), ("elo", 0.0), ("ehi", 128.0)):
-        ts(R(nm), R("vb"), v, Op.is_equal)
-    low_bits(1)
-    waits_of(1)
+    turn(R("km"), Q)
+    act(R("xr"), R(BA, 0, B), Act.Copy)
+    act(R("mo", 3 * B, 4 * B), R(BA, 0, B), Act.Identity, -6.5)
+    send(nxt, R("mi", 3 * B, 4 * B), R("mo", 3 * B, 4 * B), "ck0")
+    iota(R("rd"), [[0, EQ[7]]], 0, 0)
+    iota(R("eq"), [[0, EQ[7]]], int(TOP), 0)
     ts(R("idb"), R("vc"), 0.0, Op.is_equal)
-    ts(R("nid"), R("vc"), 0.0, Op.is_equal, -1.0, Op.mult)
-    ts(R("se0"), R("va"), 0.0, Op.is_equal)
-    ts(R("se1"), R("va"), 1.0, Op.is_equal)
+    cp(S7("o0"), SEG)
+    ts(R("se0"), R("va"), 0.0, Op.is_equal, 0.5, Op.mult)
+    ts(R("se1"), R("va"), 1.0, Op.is_equal, 0.5, Op.mult)
     ts(R("s15"), R("va"), 15.0, Op.is_equal, 256.0, Op.mult)
-    tt(R("sd"), R("se1"), R("se0"), Op.subtract)
-    fill(R("neg"), -1.0)
-    fill(R("onb"), 1.0)
-    fill(R("da", 51, 52), -LO / 128)
-    fill(R("da", 58, 59), 9.0 / 128)
+    ts(R("nid"), R("vc"), 0.0, Op.is_equal, -1.0, Op.mult)
+    ts(R("n2d"), R("vc"), 0.0, Op.is_equal, -2.0, Op.mult)
+    mm(R(BP, 0, 128), R("idb"), R("se1"), True, False)
+    mm(R(BP, 0, 128), R("nid"), R("se0"), False, True)
+    put(slot(4), M32)
+    put(slot(5), -M32)
+    put(R("pb", P0, P0 + 1), 0.0)
+    put(R("da", 51, 52), (448 - LO) / 64)
+    put(R("da", 58, 59), 9.0 / 64)
+    put(R("em", E0 - B, E0 + 30 * B, 5 * B), 2 * TOP)
+    put(R("dx", 0, 31, 5), 56 * ES)
+    put(R("ob", 555, 556), 0.0)
+    put(R("am", 0, 1), 9.0 - 8200.0)
+    low_bits(0)
+    waits_of(0)
+    low_bits(1)
+    ts(R("fm", B, 2 * B, p=16), FM, 8.0, Op.add)
     ts(slot(0, 1), S7("iw"), 16.0, Op.mult, LO, Op.add)
-    ts(S7("cwn"), S7("iw"), -1.0 / 4096, Op.mult, -W / 4096.0, Op.add)
-    fill(R("ob", B - 1, B), 0.0)
-    fill(R("am", 0, 1), 9.0 - 8200.0)
-    fill(R("dt"), 0.0)
-    low_bits(2)
-    waits_of(2)
-    fill(R("mo", 2 * B, 3 * B), LO)
-    fill(R("eq"), 4096.0)
-    fill(R("rd"), 0.0)
-    fill(R("rd", 0, 7 * B, B), 4096.0)
+    ts(R("dx", 2, 33, 5), S7("iw"), 16.0, Op.mult, DUMP + LO - 7.5, Op.add)
+    ts(sc(0), sc(2), ES, Op.mult)
+    ts(sc(1), sc(2), 1.0 / 256, Op.mult)
+    act(R("sd"), R(BP, 0, 128), Act.Copy)
 
     def gains(n, k):
-        SZ, zall, G8 = R(BS, 0, 8, p=B), R("zo", B * n, B * n + B), R("gb", 0, 128, 16)
+        SZ, zall, G8 = R(BB, 256, 264, p=B), R("zo", B * n, B * n + B), R("gb", 0, 128, 16)
         if k == 0:
             mm(SZ, zall, G8, True, True)
         elif k == 1:
@@ -287,19 +310,55 @@ def rank_program(g, core, T, topo):
         e = 16 * j + 16 if j < 3 else 64 + B
         send(cores[(rank - j) % NR], R("di", 16 * j, e), R("dt", 16 * j, e), "tp%d" % j)
 
+    def masks(n):
+        if n < STEPS - 1:
+            mm(R(BL, 0, 2 * B), F16, R("fm", p=16), True, False)
+            mm(Q, F16, FM, True, False)
+        mm(KM, R("neg", p=1), R("vc", 0, B, p=1), True, False)
+
+    def keys():
+        scan(R("km"), R("kk"), KM, 0.0, Op.mult, Op.add)
+
+    def own_key():
+        ts(S7("kb"), SEG, sc(0), Op.mult, -56 * ES, Op.add)
+
+    def compare():
+        if WDE == 1:
+            act(R("wdb"), IND(R("wt", 0, W), S7("dof0")), Act.Copy)
+        for q in range(7):
+            L = 16 * q + 16
+            act(R("eq", EQ[q + 1] - L, EQ[q + 1]), R(BK, 0, L), Act.Abs, R("kb", q, q + 1), scale=-ES)
+            if q == SKQ and not last:
+                turn(into(6), Q)
+                act(R("da", 2, 49, 7), slot(6), Act.Sign, -THR)
+            if q == 3 and last:
+                act(R("fs"), Q, Act.Sign, -THR)
+        act(R("dx", 3, 34, 5), S7("kb"), Act.Identity, C0 - LO + 7.5 - 56.0 / 256, scale=-1.0 / (256 * ES))
+        if not WDE:
+            act(R("wdb"), IND(R("wt", 0, W), S7("dof0")), Act.Copy)
+
+    def lowest(k):
+        if k == 3:
+            return scan(R("ob", 562, 801, 7), R("em", E0 - B, E0 + 33 * B + 1, B), R("dx", 0, 35), 0.0, Op.subtract, Op.min)
+        a, b = ((EQ[0], EQ[3]), (EQ[3], EQ[5]), (EQ[5], EQ[7]))[k]
+        st = 5 if k else 10
+        o = E0 + 560 * (2, 4, 6)[k] - st * (b - a - 1)
+        scan(R("em", o, o + st * (b - a - 1) + 1, st), R("rd", a, b), R("eq", a, b), TOP, Op.max, Op.min)
+
     for n in range(STEPS):
-        last = n == STEPS - 1
-        y, zo, z = R("zi", B * n, B * n + B), B * n, R("zi", B * n + B, B * n + 2 * B)
+        first, last = n == 0, n == STEPS - 1
+        zo = B * n
+        y, z = R("zi", zo, zo + B), R("zi", zo + B, zo + 2 * B)
         m0 = 4 * B * n
         part = lambda name, k: R(name, m0 + k * B, m0 + k * B + B)
-        fetch = S7("o0") if n == 0 else R("oi", 16 * n - 16, 16 * n - 9)
-        if n == 0:
+        fetch = S7("o0") if first else R("oi", 16 * n - 16, 16 * n - 9)
+        if first:
             tt(R("ui"), IND(R("ili"), fetch), R("xr"), Op.add)
             act(part("mo", 0), IND(R("ili"), fetch), Act.Identity, LO - 15.5)
+            waits_of(1)
             ts(R("u5"), R("ui"), 31, Op.bitwise_and)
-            low_bits(3)
             ts(part("mo", 1), R("u5"), -15.5, Op.add)
-            waits_of(3)
+            low_bits(2)
         else:
             landed("of%d" % (n - 1), prv, R("oi", 16 * n - 16, 16 * n))
             tt(part("mo", 1), IND(R("wt", 0, W), fetch), R("xr"), Op.add)
@@ -308,41 +367,53 @@ def rank_program(g, core, T, topo):
             cp(IND(R("xt"), R("oi", 16 * n - 8, 16 * n - 1)), y)
             if not last:
                 act(part("mo", 3), R("xr"), Act.Identity, R("av", n, n + 1))
-        mw = 4 * B if 0 < n < STEPS - 1 else 3 * B
+        mw = 3 * B if first or last or CK else 4 * B
         send(nxt, R("mi", m0, m0 + mw), R("mo", m0, m0 + mw), "ea%d" % n)
-        act(R(BL, 0, B), y, Act.Relu, -1.0, scale=2.0)
-        if n > 0:
+        act(R("sy"), y, Act.Sign)
+        if not first:
             gains(n - 1, 1)
-        terms = (1, 0, 2) if n > 0 else (0, 1)
+        terms = (0, 1) if first else (1, 0, 2)
         for pb, lo, hi, od in ((R(BO, 0, 56), "olo", "ohi", "sod"), (R(BE, 0, 56), "elo", "ehi", "sev")):
             for k in terms:
                 a = m0 + k * B
                 mm(pb, R(lo), R("mo", a, a + B, 2), k == terms[0], False)
                 mm(pb, R(hi), R("mo", a + 1, a + B, 2), False, k == terms[-1])
-            ts(R(od), pb, -C0 if n > 0 else LO - C0, Op.add)
+            ts(R(od), pb, LO - C0 if first else -C0, Op.add)
+        if first:
+            low_bits(3)
+            cp(R("wt", IL[3], W), R("an", IL[3], W))
+            fill(R("rd", 0, EQ[3], 56), TOP)
+            fill(R("rd", EQ[3], EQ[7], B), TOP)
+            masks(0)
         for a, b in zip(CH, CH[1:]):
             act(R("vo", 8 * a, 8 * b), IND(R("xt"), R("sod", a // 2, b // 2)), Act.Copy)
-        DL, L0, Q, KM, PK = R(BL, B, 2 * B), R(BL, 2 * B, 3 * B), R(BQ, 0, B), R(BK, 0, B), R(BP, 0, B)
-        DE, DZ = R(BO, 128, 128 + EARLY), R(BE, 128, 128 + B - EARLY)
-        if n > 0:
+        if first:
+            waits_of(2)
+        else:
             gains(n - 1, 2)
-            if n > 5:
-                gains_home(n - 5)
+            if last:
+                gains_home(2)
+            elif CK:
+                ensure("G", {"S": cnt["S"] - CK + 1})
+                send(nxt, part("mi", 3), part("mo", 3), "ck%d" % n)
+        mm(DL, R("sd"), part("mo", 0), last, False)
+        mm(L0, R("se0"), part("mo", 0), False, False)
+        mm(L0, R("se1"), part("mo", 0), False, True)
         if not last:
-            mm(DL, F16, FM, True, False)
-        mm(DL, R("sd"), part("mo", 0), last, True)
-        if not last:
-            mm(L0, F16, FM8, True, False)
-        mm(L0, R("se0"), part("mo", 0), last, True)
-        mm(DE, R("nid"), R("zi", B * n, B * n + EARLY), True, False)
-        mm(DZ, R("nid"), R("zi", B * n + EARLY, B * n + B), True, False)
-        if not last:
-            mm(Q, F16, FM, True, False)
             mm(Q, R("idb"), part("mo", 3), False, False)
-        mm(KM, F16, FM, True, False)
+        halves = ((0, EARLY, BO), (EARLY, B, BE))
+        for a, b, bank in halves:
+            mm(R(bank, 128, 128 + b - a), R("nid"), R("zi", zo + a, zo + b), True, False)
+            mm(R(BA if a else bank, 256, 256 + b - a), R("n2d"), R("zi", zo + a, zo + b), a > 0, False)
+            mm(R(BA if a else bank, 256, 256 + b - a), R("idb"), R("sy", a, b), False, False)
+
+        def places(out):
+            for k in range(3):
+                mm(out, R("s15"), part("mi", k), False, k == 2)
         landed("ea%d" % n, prv, R("mi", m0, m0 + mw))
-        for k in range(3):
-            mm(KM, R("s15"), part("mi", k), False, k == 2)
+        pke = PKE[core not in topo.cores_of(prv)]
+        if pke >= 2:
+            places(KM)
         done = [0]
 
         def greatest(upto):
@@ -354,89 +425,103 @@ def rank_program(g, core, T, topo):
             tt(R("mn2", 8 * a, 8 * b), IND(R("xt"), R("sev", a // 2, b // 2)), R("vo", 8 * a, 8 * b), Op.min)
             greatest(a)
         greatest(B)
-        for a, b, D in ((0, EARLY, DE), (EARLY, B, DZ)):
+        for a, b, bank in halves:
             m = R("mx", 8 * a + 7, 8 * b, 8)
-            mm(D, R("idb"), m, False, True)
-            act(R("sg", a, b), m, Act.Sign)
-            act(R("zo", zo + a, zo + b), D, Act.Abs)
-            if a == 0:
-                mm(R(BQ, a, b), R("gn"), R("sg", a, b), last, False)
+            mm(R(bank, 128, 128 + b - a), R("idb"), m, False, a > 0)
+            mm(R(BA if a else bank, 256, 256 + b - a), R("idb"), m, False, True)
+            act(R("s0", a, b), m, Act.Sign, -0.5)
+            if a:
+                keys()
+            act(R("zo", zo + a, zo + b), R(bank, 128, 128 + b - a), Act.Abs)
+            if a:
+                send(nxt, z, R("zo", zo, zo + B), "zr%d" % n)
                 if not last:
-                    mm(R(BQ, a, b), R("gb"), R("zo", zo + a, zo + b), False, False)
-        send(nxt, z, R("zo", zo, zo + B), "zr%d" % n)
+                    turn(into(1), DL)
+                own_key()
+                ts(R("s1", a, b), R(BA, 256, 256 + b - a), 0.5, Op.is_gt, -0.5, Op.add)
+            else:
+                act(R("s1", a, b), R(bank, 256, 256 + b - a), Act.Sign, -0.5)
+                if pke < 2:
+                    places(KM)
+            mm(R(BQ, a, b), R("gn"), R("s0", a, b), last and not a, False)
+            if last:
+                mm(R(BQ, a, b), R("g2" if a else "gp"), R("s1", a, b), False, a > 0)
+            else:
+                mm(R(BQ, a, b), R("g2" if a else "gp"), R("s1", a, b), False, False)
+                mm(R(BQ, a, b), R("gb"), R("zo", zo + a, zo + b), False, a > 0)
         if not last:
-            turn(into(1), DL)
-        tt(R("ge"), R("mx", 7, 8 * B, 8), R(BL, 0, B), Op.is_gt)
-        if last:
-            mm(R(BQ, 0, EARLY), R("gp"), R("ge", 0, EARLY), False, True)
-            mm(R(BQ, EARLY, B), R("gn"), R("sg", EARLY, B), True, False)
-            mm(R(BQ, EARLY, B), R("gp"), R("ge", EARLY, B), False, True)
-        else:
-            mm(R(BQ, EARLY, B), R("gn"), R("sg", EARLY, B), False, False)
-            mm(Q, R("gp"), R("ge"), False, False)
-            mm(R(BQ, EARLY, B), R("gb"), R("zo", zo + EARLY, zo + B), False, True)
             turn(into(2), L0)
-        turn(R("km"), KM)
-        mm(PK, R("neg", p=1), R("vc", 0, B, p=1), True, False)
-        for k in range(3):
-            mm(PK, R("s15"), part("mi", k), False, k == 2)
-        ts(S7("dof0"), SEG, 1.0 / 256, Op.mult, -C0, Op.add)
-        for q in range(7):
-            L = 16 * q + 16
-            act(R("eq", B * q + B - L, B * q + B), R(BP, 0, L), Act.Abs, R("km", 16 * q + 15, 16 * q + 16), scale=-1.0)
-        thr = -7 * HI - 64
+        ts(S7("dof0"), SEG, sc(1), Op.mult, -C0, Op.add)
+        compare()
+        o0 = 24 * n
+        rze = not (first or last) and RZE[core not in topo.cores_of(prv)]
+        landed("zr%d" % n, prv, z)
+
+        def new_waits():
+            if WDE == 2:
+                tt(R("rz"), IND(R("wt", 0, W), S7("dof0")), z, Op.add)
+            else:
+                mm(R(BO, 0, B), R("idb"), R("wdb"), True, True)
+                tt(R("rz"), z, R(BO, 0, B), Op.add)
+        joint = not (first or last) and LOW[3] != "d"
+
+        def offsets(a, b):
+            ts(R("oo", o0 + a, o0 + b), R("ob", 30 + 35 * a, 31 + 35 * (b - 1), 35), 7.5 - LO, Op.add)
         if not last:
-            turn(into(6), Q)
-            ts(S7("nk"), SEG, -2.0 ** -20, Op.mult, C0 / 4096, Op.add)
-            ts(R("da", 2, 49, 7), slot(6), thr, Op.is_ge)
+            def lows(c):
+                for k in range(4):
+                    if LOW[k] == c:
+                        lowest(k)
+            lows("a")
             ts(slot(3), slot(6), M16, Op.add, -M16, Op.add)
-            tt(S7("nk"), S7("nk"), S7("iw"), Op.subtract)
-            scan(R("ob", 0, 49), R("da", 0, 49), R("pb", P0, P0 + 16 * 48 + 1, 16), 0.0, Op.mult, Op.add)
-            scan(R("ob", 55, 105), R("db", 0, 50), R("pb", P0, P0 + 16 * 49 + 1, 16), 0.0, Op.mult, Op.add)
-            ts(R("oo", 16 * n, 16 * n + 16), R("ob", 6, B, 7), 7.5 - LO, Op.add)
-            send(nxt, R("oi", 16 * n, 16 * n + 16), R("oo", 16 * n, 16 * n + 16), "of%d" % n)
+            lows("b")
+            scan(R("ob", 275, 521, 5), R("db", 0, 50), R("pb", P0, P0 + 16 * 49 + 1, 16), 0.0, Op.mult, Op.add)
+            lows("B")
+            scan(R("ob", 0, 241, 5), R("da", 0, 49), R("pb", P0, P0 + 16 * 48 + 1, 16), 0.0, Op.mult, Op.add)
+            lows("c")
+            if rze:
+                new_waits()
+            offsets(0, 23 if joint else 16)
+            send(nxt, R("oi", 16 * n, 16 * n + 16), R("oo", o0, o0 + 16), "of%d" % n)
+            if n == 6:
+                gains_home(1)
             mm(R(BQ, 128, 137), R("onb"), R("da", 2, 59, 7), True, True)
+            lows("d")
         else:
-            ts(R("fs"), Q, thr, Op.is_ge)
-            ts(S7("nk"), SEG, -2.0 ** -20, Op.mult, C0 / 4096, Op.add)
-            tt(R("fd"), R("fs"), DL, Op.mult)
-            tt(S7("nk"), S7("nk"), S7("iw"), Op.subtract)
-            tt(R("fl"), R("fd"), L0, Op.add)
-        gains(n, 0)
-        act(R("wdb"), IND(R("wt", 0, W), S7("dof0")), Act.Copy)
-        mm(R(BK, 128, 128 + B), R("idb"), R("wdb"), True, True)
-        if not last:
-            act(R("jk", 0, 9), R(BQ, 128, 137), Act.Copy, acc=R("ac", 0, 1))
-            act(R("fa", 0, 1), R("ac", 0, 1), Act.Identity, 24.5, scale=-1.0)
-            act(R("av", n + 1, n + 2), R("ac", 0, 1), Act.Identity, R("fa", 0, 1))
-        else:
+            gains(n, 0)
             gains(n, 1)
             gains(n, 2)
-        scan(R("em", 0, 448), R("rd", 0, 448), R("eq", 0, 448), 4096.0, Op.max, Op.min)
-        if last:
+            lowest(0)
+            tt(R("fd"), R("fs"), DL, Op.mult)
+            lowest(1)
+            tt(R("fl"), R("fd"), L0, Op.add)
+            lowest(2)
             ts(R("dt", 64, 64 + B), R("fl"), 1.0 / 32, Op.mult, -LO / 32, Op.add)
-        scan(R("em", 448, 784), R("rd", 448, 784), R("eq", 448, 784), 4096.0, Op.max, Op.min)
-        if last:
+            lowest(3)
             gains_home(3)
-        X1, X2 = R(BP, 128, 128 + B), R(BX, 0, B)
-        if not last:
-            if n == 0:
-                landed("ck", prv, part("mi", 3))
-            mm(X1, R("idb"), part("mi", 3), True, False)
-            mm(X2, R("idb"), part("mi", 3), True, False)
-        tt(S7("tp8"), R("em", B - 1, 7 * B, B), S7("nk"), Op.add)
-        landed("zr%d" % n, prv, z)
-        tt(S7("mn"), S7("tp8"), S7("cwn"), Op.max)
-        tt(R("rz"), z, R(BK, 128, 128 + B), Op.add)
-        ts(S7("doff"), S7("mn"), -4096.0, Op.mult)
+        X1, X2 = R(BA, 0, B), R(BB, 0, B)
+        if not rze:
+            new_waits()
+        if not joint:
+            offsets(16, 23)
         ts(R("ry"), R("rz"), 31, Op.bitwise_and)
-        cp(IND(R("wt"), S7("doff")), R("ry"))
-        if not last:
-            mm(X1, R("gb"), z, False, True)
-            mm(X2, R("gb"), z, False, False)
-            act(R("fx"), X1, Act.Identity, 14336.0, scale=-1.0)
-            mm(X2, R("idb"), R("fx"), False, True)
-            act(R("xr"), X2, Act.Identity, -14344.0)
+        cp(IND(R("wt"), R("oo", o0 + 16, o0 + 23)), R("ry"))
+        if last:
+            break
+        if first or CK:
+            landed("ck%d" % n, prv, part("mi", 3))
+        for X in (X1, X2):
+            mm(X, R("idb"), part("mi", 3), True, False)
+        for X in (X1, X2):
+            mm(X, R("gb"), z, False, X is X1)
+        act(R("jk", 0, 9), R(BQ, 128, 137), Act.Copy, acc=R("ac", 0, 1))
+        act(R("fx", 0, B), X1, Act.Identity, 14336.0, scale=-1.0)
+        mm(X2, R("idb"), R("fx", 0, B), False, True)
+        act(R("fa", 0, 1), R("ac", 0, 1), Act.Identity, 24.5, scale=-1.0)
+        act(R("xr"), X2, Act.Identity, -14344.0)
+        act(R("av", n + 1, n + 2), R("ac", 0, 1), Act.Identity, R("fa", 0, 1))
+        masks(n + 1)
+        gains(n, 0)
 
     dma("Y", T.yw[:, :], T.wt[:, 0:W], R("wt", 0, W)[1], [])
     dma("S", T.yy[:, :], T.zi[:, 8 * B:9 * B], z[1], [])
@@ -446,10 +531,10 @@ def rank_program(g, core, T, topo):
             landed("tp%d" % j, cores[(rank + j) % NR], R("di", 16 * j, 16 * j + 16 if j < 3 else 64 + B))
         for h in range(2):
             a = 16 * j + 8 * h
-            mm(R(BQ, 0, B, p=8), R("dt" if j == 0 else "di", a, a + 8, p=B), idq, a == 0, a == 56)
+            mm(R(BK, 0, B, p=8), R("dt" if j == 0 else "di", a, a + 8, p=B), idq, a == 0, a == 56)
     act(R("fy"), R("di", 64, 64 + B), Act.Copy)
     dma("S", T.yl[:, :], T.fy[0:128:16, :], R("fy")[1], [])
-    tt(R("ft", p=8), R("tki", p=8), R(BQ, 0, B, p=8), Op.add)
+    tt(R("ft", p=8), R("tki", p=8), R(BK, 0, B, p=8), Op.add)
     ts(R("fu", p=8), R("ft", p=8), 4095, Op.bitwise_and)
     cp(R("fv", p=8), R("fu", p=8))
     dma("Y", T.yt[:, :], T.fv[0:8, :], R("fv")[1], [])

from concourse.mybir import AluOpType as Op, ActivationFunctionType as Act

NR, B, W, STEPS = 4, 112, 1920, 8
OFF = float(2 ** 23)
M16, M32 = float(3 * 2 ** 26), float(3 * 2 ** 27)
LO = 6144.0
C0 = 2 * LO - 15.5
HI = 8192.0
CH = (0, 12, 32, 56, 84, B)
SC = (0, 32, 56, 84, B)
EARLY = 56
PKE, WDE, LOW, CK, KL = (2, 0), 2, "aacd", 1, 1
SKQ = 5
RZE = (0, 0)
UP, TOP, ES = float(2 ** 30), float(2 ** 22), float(2 ** 14)
THR = -7 * HI - 64
LD = (0, 960, W)
IL = (0, 480, 960, 1440, W)
DUMP = 2048
WT = DUMP + 16 * B
P0 = 89
EQ = (0, 56, 112, 168, 280, 392, 504, 616)
E0 = 550

SCRATCH = {}
for _names, _w, _t in (
        ("xt", W, "bfloat16"), ("wt", WT, "bfloat16"), ("ili an", W, "int32"),
        ("tki lni ui u5 rz ry ft fu", B, "int32"), ("ip", 8, "int32"), ("p15", 8, "int32"),
        ("km fy fv", B, "float32"), ("pf ac sc up kb", 8, "float32"), ("ka kc kk", B, "bfloat16"), ("i16", 32, "float32"), ("dx xo", 40, "float32"),
        ("t5b l32 xr wdb sy s0 s1 wn r3 fs fd fl", B, "bfloat16"), ("fm fx", 2 * B, "bfloat16"),
        ("va vb vc ve e8 vf onb neg f16 idb nid n2d gb g2 gp gn se0 se1 sd s15 elo ehi olo ohi", 128, "bfloat16"),
        ("iw dd mn av am jk", 16, "float32"), ("fa fz", 8, "bfloat16"),
        ("doff dof0", 8, "uint16"), ("o0", 16, "uint16"), ("idl", 32, "uint16"), ("sev sod", 56, "uint16"),
        ("rd eq", EQ[7], "bfloat16"), ("em", 38 * B, "bfloat16"), ("r8", 8 * 32, "bfloat16"), ("vo mn2 mx", 8 * B, "bfloat16"),
        ("pb", 880, "float32"), ("da db", 64, "bfloat16"), ("ob", 808, "float32"),
        ("zi", 9 * B, "bfloat16"), ("zo", 8 * B, "bfloat16"),
        ("mo mi", 8 * 4 * B, "bfloat16"),
        ("oo", 8 * 24, "uint16"), ("oi", 8 * 16, "uint16"),
        ("dt di", 64 + B, "bfloat16")):
    for _n in _names.split():
        SCRATCH[_n] = ("sbuf", [128, _w], _t)
PSUM = ["b%d" % i for i in range(8)]
for _n in PSUM:
    SCRATCH[_n] = ("psum", [128, 512], "float32")
SEMAPHORES = (["sV", "sS", "sP", "sG", "lsem", "tp1", "tp2", "tp3"] + ["%s%d" % (a, i) for a in ("ck", "zr", "ea", "of") for i in range(8)]
              + ["d%d" % i for i in range(16)])


def rank_program(g, core, T, topo):
    rank = T.rank_of(core)
    if rank is None:
        return
    cores = T.cores
    nxt, prv = cores[(rank + 1) % NR], cores[(rank - 1) % NR]
    V, S, P = g.vector, g.scalar, g.tensor
    queues = {"V": V, "S": S, "P": P, "G": g, "Y": g.sync}
    sems = {"V": "sV", "S": "sS", "P": "sP", "G": "sG"}
    cnt = {"V": 0, "S": 0, "P": 0, "G": 0}
    know = {q: {} for q in queues}
    clocks = {}
    log = {}

    def ensure(q, need):
        need = {x: i for x, i in need.items() if know[q].get(x, 0) < i}
        for x in list(need):
            if any(y != x and clocks.get((y, j), {}).get(x, 0) >= need[x] for y, j in need.items()):
                del need[x]
        for x, i in need.items():
            queues[q].wait_ge(T.sem[sems.get(x, x)], i)
            for y, j in clocks.get((x, i), {}).items():
                know[q][y] = max(know[q].get(y, 0), j)
            know[q][x] = max(know[q].get(x, 0), i)

    def deps(q, reads, writes):
        need = {}
        for regs, wr in ((reads, False), (writes, True)):
            for name, cols in regs:
                ps = name in PSUM
                for (c, x, i, w) in log.get(name, []):
                    if x == q:
                        if not (w and q != "P" and c & cols):
                            continue
                    elif not (ps or (c & cols and (w or wr))):
                        continue
                    need[x] = max(need.get(x, 0), i)
        return need

    def note(x, i, reads, writes):
        for name, cols in writes:
            log[name] = [e for e in log.get(name, []) if e[0] & ~cols] + [(cols, x, i, True)]
        for name, cols in reads:
            log[name] = [e for e in log.get(name, []) if e[3] or e[1] != x or e[0] & ~cols] + [(cols, x, i, False)]

    def emit(q, reads, writes, fn):
        ensure(q, deps(q, reads, writes))
        fn().then_inc(T.sem[sems[q]], 1)
        cnt[q] += 1
        c = dict(know[q])
        c[q] = cnt[q]
        clocks[(q, cnt[q])] = c
        note(q, cnt[q], reads, writes)

    def R(name, a=0, b=None, st=1, p=128):
        if b is None:
            b = SCRATCH[name][1][1]
        t = T[name]
        cols = (1 << b) - (1 << a) if st == 1 else sum(1 << c for c in range(a, b, st))
        return (t[0:p, a:b] if st == 1 else t[0:p, a:b:st], [(name, cols)], [])

    def IND(win, off):
        return (win[0].indirect(off[0]), win[1], off[1])

    def rd(*ops):
        return [r for o in ops if isinstance(o, tuple) for r in o[1] + o[2]]

    def ap(o):
        return o[0] if isinstance(o, tuple) else o

    def tt(out, a, b, op):
        emit("V", rd(a, b) + out[2], out[1], lambda: V.tensor_tensor(out=out[0], in0=a[0], in1=b[0], op=op))

    def ts(out, a, s1, op0, s2=None, op1=None):
        if op1 is None:
            emit("V", rd(a, s1) + out[2], out[1], lambda: V.tensor_scalar(out=out[0], in0=a[0], scalar1=ap(s1), scalar2=None, op0=op0))
        else:
            emit("V", rd(a, s1, s2) + out[2], out[1], lambda: V.tensor_scalar(out=out[0], in0=a[0], scalar1=ap(s1), scalar2=ap(s2), op0=op0, op1=op1))

    def cp(out, a):
        emit("V", rd(a) + out[2], out[1], lambda: V.tensor_copy(out=out[0], in_=a[0]))

    def scan(out, d0, d1, init, op0, op1):
        emit("V", rd(d0, d1), out[1], lambda: V.tensor_tensor_scan(out=out[0], data0=d0[0], data1=d1[0], initial=init, op0=op0, op1=op1))

    def fill(out, v):
        emit("V", [], out[1], lambda: V.memset(out[0], v))

    def act(out, a, f, bias=None, acc=None, scale=None):
        kw = {}
        if scale is not None:
            kw["scale"] = ap(scale)
        if bias is not None:
            kw["bias"] = ap(bias)
        if acc is not None:
            kw["accum_out"] = acc[0]
        emit("S", rd(a, bias, scale), out[1] + (acc[1] if acc is not None else []),
             lambda: S.activation(out=out[0], in_=a[0], func=f, **kw))

    def mm(out, l, r, start, stop):
        emit("P", rd(l, r), out[1], lambda: P.matmul(out[0], l[0], r[0], start, stop))

    def iota(out, pat, base, cm):
        if SCRATCH[out[1][0][0]][2] == "int32":
            emit("G", [], out[1], lambda: g.iota(out[0], pat, base, cm))
        else:
            emit("G", [], out[1], lambda: g.iota(out[0], pat, base, cm, allow_small_or_imprecise_dtypes=True))

    dma_all = []

    def dma(q, out, src, reads, writes):
        name = "d%d" % len(dma_all)
        ensure(q, deps(q, reads, writes))
        queues[q].dma_start(out=out, in_=src).then_inc(T.sem[name], 16)
        c = dict(know[q])
        c[name] = 16
        clocks[(name, 16)] = c
        note(name, 16, reads, writes)
        dma_all.append(name)

    sent = [0]

    def send(dst, out, src, sem):
        ensure("G", deps("G", src[1], []))
        rid, pid = topo.addr(dst, core)
        g.remote_dma(out_ap=out[0], in_ap=src[0], remote_sem=T.sem[sem], local_sem=T.sem.lsem, pid=pid, routing_id=rid,
                     dma_engine_mask=topo.mask(core, dst))
        sent[0] += len(topo.engines(core, dst))

    def landed(sem, src, reg):
        note(sem, len(topo.engines(src, core)), [], reg[1])

    BQ, BL, BK, BP, BO, BE, BA, BB = PSUM
    S7 = lambda name: R(name, 0, 7)
    SEG = R("km", 15, B, 16)
    slot = lambda k, q0=0: R("pb", P0 + 16 * k + B * q0, P0 + 16 * k + B * (q0 + 6) + 1, B)
    into = lambda k: R("pb", P0 + 16 * k - 105, P0 + 16 * k - 105 + 7 * B, 7)
    F16, FM = R("f16", p=16), R("fm", 0, B, p=16)
    DL, L0, Q, KM = R(BL, 0, B), R(BL, B, 2 * B), R(BQ, 0, B), R(BK, 0, B)
    sc = lambda k: R("sc", k, k + 1)

    def turn(out, src):
        scan(out, R("r3"), src, 0.0, Op.min, Op.max)

    dma("Y", T.tki[0:8, :], T.tk0[:, :], [], R("tki")[1])
    dma("S", T.lni[0:8, :], T.ln0[:, :], [], R("lni")[1])
    for a, b in zip(LD, LD[1:]):
        dma("Y", T.ili[:, a:b], T.il[:, a:b], [], R("ili", a, b)[1])
    dma("Y", T.xt[:, :], T.xw[:, :], [], R("xt")[1])
    dma("Y", T.zi[:, 0:B], T.y0[:, :], [], R("zi", 0, B)[1])

    iota(R("ve", p=8), [[-1, 8], [0, 16]], 0, 1)
    iota(R("vf", p=16), [[0, 8], [-1, 16]], 0, 1)
    iota(R("ip"), [[0, 8]], 0, 1)
    iota(R("i16"), [[16, 32]], 0, 0)
    iota(R("vb"), [[-16, 8], [128, 2], [-2, 8]], 0, 1)
    iota(R("va"), [[-16, 8], [0, 16]], 0, 1)
    iota(R("vc"), [[-1, 128]], 0, 1)
    iota(R("dt"), [[0, 64 + B]], 0, 0)
    iota(R("mo", 2 * B, 3 * B), [[0, B]], int(LO), 0)

    def put(out, v):
        act(out, R("onb", 0, out[0].shape[1]), Act.Identity, v, scale=0.0)
    fill(R("onb"), 0.5)
    fill(R("r3"), 2 * OFF)
    fill(R("r8"), 255.0)
    fill(R("neg"), -1.0)
    fill(R("r3", 0, B, 16), -2 * OFF)
    fill(R("r8", 0, 8 * 32, 8), 0.0)
    put(R("da"), 1.0)
    put(R("db"), 0.0)
    put(R("dx"), TOP)
    put(R("em", E0 - B, E0 + 33 * B + 1, B), 0.0)
    for k, v in ((0, 0.0), (1, 0.0), (3, -1.0), (6, -1.0)):
        put(R("da", k, 49, 7), v)
    for k, v in ((0, 1.0), (4, 2.0), (5, 1.0), (6, -0.5)):
        put(R("db", k, 50, 7), v)
    E8 = R("e8", p=8)
    ts(E8, R("ve", p=8), 0.0, Op.is_equal)
    ts(F16, R("vf", p=16), 0.0, Op.is_equal)
    ts(FM, R("vf", 0, B, p=16), 0.0, Op.not_equal, -OFF, Op.mult)
    ts(R("p15"), R("ip"), 15, Op.bitwise_and)
    mm(R(BB, 0, 128), E8, E8, True, True)
    ts(R("ka", p=16), R("vf", 0, B, p=16), 0.0, Op.not_equal)
    cp(R("pf"), R("p15"))
    ts(R("kc", p=16), R("vf", 0, B, p=16), -1.0, Op.is_equal, UP, Op.mult)
    ts(R("idl"), R("i16"), R("pf", 0, 1), Op.add)
    ts(R("iw"), R("i16", 0, 16), R("pf", 0, 1), Op.add)
    ts(sc(2), R("pf", 0, 1), 15.0, Op.is_equal, 1.0 / UP, Op.max)
    ts(R("u5", p=8), R("tki", p=8), 31, Op.bitwise_and)
    ts(R("l32", p=8), R("lni", p=8), 32.0, Op.mult)
    cp(R("t5b", p=8), R("u5", p=8))
    for nm, v in (("gb", 1.0), ("gp", HI / 2), ("g2", HI), ("gn", -HI / 2)):
        act(R(nm), R(BB, 0, 128), Act.Copy, scale=v)
    mm(R(BP, 0, B), F16, R("ka", p=16), True, False)
    mm(R(BP, 0, B), F16, R("kc", p=16), False, True)
    mm(Q, F16, FM, True, False)
    mm(Q, E8, R("l32", p=8), False, False)
    mm(Q, E8, R("t5b", p=8), False, True)
    mm(R(BA, 0, B), E8, R("t5b", p=8), True, True)
    act(R("kk"), R(BP, 0, B), Act.Copy)
    for nm, v in (("olo", 1.0), ("ohi", 129.0), ("elo", 0.0), ("ehi", 128.0)):
        ts(R(nm), R("vb"), v, Op.is_equal)

    def low_bits(j):
        a, b = IL[j], IL[j + 1]
        ts(R("an", a, b), R("ili", a, b), 31, Op.bitwise_and)

    def waits_of(j):
        a, b = IL[j], IL[j + 1]
        act(R("wt", a, b), IND(R("an", a, b), R("idl", 0, (b - a) // 16)), Act.Copy)

    turn(R("km"), Q)
    act(R("xr"), R(BA, 0, B), Act.Copy)
    act(R("mo", 3 * B, 4 * B), R(BA, 0, B), Act.Identity, -6.5)
    send(nxt, R("mi", 3 * B, 4 * B), R("mo", 3 * B, 4 * B), "ck0")
    iota(R("rd"), [[0, EQ[7]]], 0, 0)
    iota(R("eq"), [[0, EQ[7]]], int(TOP), 0)
    ts(R("idb"), R("vc"), 0.0, Op.is_equal)
    cp(S7("o0"), SEG)
    ts(R("se0"), R("va"), 0.0, Op.is_equal, 0.5, Op.mult)
    ts(R("se1"), R("va"), 1.0, Op.is_equal, 0.5, Op.mult)
    ts(R("s15"), R("va"), 15.0, Op.is_equal, 256.0, Op.mult)
    ts(R("nid"), R("vc"), 0.0, Op.is_equal, -1.0, Op.mult)
    ts(R("n2d"), R("vc"), 0.0, Op.is_equal, -2.0, Op.mult)
    mm(R(BP, 0, 128), R("idb"), R("se1"), True, False)
    mm(R(BP, 0, 128), R("nid"), R("se0"), False, True)
    put(slot(4), M32)
    put(slot(5), -M32)
    put(R("pb", P0, P0 + 1), 0.0)
    put(R("da", 51, 52), (448 - LO) / 64)
    put(R("da", 58, 59), 9.0 / 64)
    put(R("em", E0 - B, E0 + 30 * B, 5 * B), 2 * TOP)
    put(R("dx", 0, 31, 5), 56 * ES)
    put(R("ob", 555, 556), 0.0)
    put(R("am", 0, 1), 9.0 - 8200.0)
    low_bits(0)
    waits_of(0)
    low_bits(1)
    ts(R("fm", B, 2 * B, p=16), FM, 8.0, Op.add)
    ts(slot(0, 1), S7("iw"), 16.0, Op.mult, LO, Op.add)
    ts(R("dx", 2, 33, 5), S7("iw"), 16.0, Op.mult, DUMP + LO - 7.5, Op.add)
    ts(sc(0), sc(2), ES, Op.mult)
    ts(sc(1), sc(2), 1.0 / 256, Op.mult)
    act(R("sd"), R(BP, 0, 128), Act.Copy)

    def gains(n, k):
        SZ, zall, G8 = R(BB, 256, 264, p=B), R("zo", B * n, B * n + B), R("gb", 0, 128, 16)
        if k == 0:
            mm(SZ, zall, G8, True, True)
        elif k == 1:
            act(R("fz", p=B), SZ, Act.Identity, 8192.0 + 15.5, scale=-1.0)
            if n < STEPS - 1:
                act(R("am", n + 1, n + 2), R("av", n + 1, n + 2), Act.Identity, -8200.0)
        else:
            mm(SZ, zall, G8, True, False)
            mm(SZ, (T.idb[0:B, 0:B], R("idb")[1], []), R("fz", p=B), False, True)
            d0 = 16 * (n % 4) + 8 * (n // 4)
            act(R("dt", d0, d0 + 8, p=B), SZ, Act.Identity, R("am", n, n + 1, p=B))

    def gains_home(j):
        e = 16 * j + 16 if j < 3 else 64 + B
        send(cores[(rank - j) % NR], R("di", 16 * j, e), R("dt", 16 * j, e), "tp%d" % j)

    def masks(n):
        if n < STEPS - 1:
            mm(R(BL, 0, 2 * B), F16, R("fm", p=16), True, False)
            mm(Q, F16, FM, True, False)
        mm(KM, R("neg", p=1), R("vc", 0, B, p=1), True, False)

    def keys():
        scan(R("km"), R("kk"), KM, 0.0, Op.mult, Op.add)

    def own_key():
        ts(S7("kb"), SEG, sc(0), Op.mult, -56 * ES, Op.add)

    def compare():
        if WDE == 1:
            act(R("wdb"), IND(R("wt", 0, W), S7("dof0")), Act.Copy)
        for q in range(7):
            L = 16 * q + 16
            act(R("eq", EQ[q + 1] - L, EQ[q + 1]), R(BK, 0, L), Act.Abs, R("kb", q, q + 1), scale=-ES)
            if q == SKQ and not last:
                turn(into(6), Q)
                act(R("da", 2, 49, 7), slot(6), Act.Sign, -THR)
            if q == 3 and last:
                act(R("fs"), Q, Act.Sign, -THR)
        act(R("dx", 3, 34, 5), S7("kb"), Act.Identity, C0 - LO + 7.5 - 56.0 / 256, scale=-1.0 / (256 * ES))
        if not WDE:
            act(R("wdb"), IND(R("wt", 0, W), S7("dof0")), Act.Copy)

    def lowest(k):
        if k == 3:
            return scan(R("ob", 562, 801, 7), R("em", E0 - B, E0 + 33 * B + 1, B), R("dx", 0, 35), 0.0, Op.subtract, Op.min)
        a, b = ((EQ[0], EQ[3]), (EQ[3], EQ[5]), (EQ[5], EQ[7]))[k]
        st = 5 if k else 10
        o = E0 + 560 * (2, 4, 6)[k] - st * (b - a - 1)
        scan(R("em", o, o + st * (b - a - 1) + 1, st), R("rd", a, b), R("eq", a, b), TOP, Op.max, Op.min)

    for n in range(STEPS):
        first, last = n == 0, n == STEPS - 1
        zo = B * n
        y, z = R("zi", zo, zo + B), R("zi", zo + B, zo + 2 * B)
        m0 = 4 * B * n
        part = lambda name, k: R(name, m0 + k * B, m0 + k * B + B)
        fetch = S7("o0") if first else R("oi", 16 * n - 16, 16 * n - 9)
        if first:
            tt(R("ui"), IND(R("ili"), fetch), R("xr"), Op.add)
            act(part("mo", 0), IND(R("ili"), fetch), Act.Identity, LO - 15.5)
            waits_of(1)
            ts(R("u5"), R("ui"), 31, Op.bitwise_and)
            ts(part("mo", 1), R("u5"), -15.5, Op.add)
            low_bits(2)
        else:
            landed("of%d" % (n - 1), prv, R("oi", 16 * n - 16, 16 * n))
            tt(part("mo", 1), IND(R("wt", 0, W), fetch), R("xr"), Op.add)
            act(part("mo", 0), IND(R("ili"), fetch), Act.Identity, LO - 15.5)
            ts(part("mo", 2), part("mo", 1), -1.0, Op.mult, LO, Op.add)
            cp(IND(R("xt"), R("oi", 16 * n - 8, 16 * n - 1)), y)
            if not last:
                act(part("mo", 3), R("xr"), Act.Identity, R("av", n, n + 1))
        mw = 3 * B if first or last or CK else 4 * B
        send(nxt, R("mi", m0, m0 + mw), R("mo", m0, m0 + mw), "ea%d" % n)
        act(R("sy"), y, Act.Sign)
        if not first:
            gains(n - 1, 1)
        terms = (0, 1) if first else (1, 0, 2)
        for pb, lo, hi, od in ((R(BO, 0, 56), "olo", "ohi", "sod"), (R(BE, 0, 56), "elo", "ehi", "sev")):
            for k in terms:
                a = m0 + k * B
                mm(pb, R(lo), R("mo", a, a + B, 2), k == terms[0], False)
                mm(pb, R(hi), R("mo", a + 1, a + B, 2), False, k == terms[-1])
            ts(R(od), pb, LO - C0 if first else -C0, Op.add)
        if first:
            low_bits(3)
            cp(R("wt", IL[3], W), R("an", IL[3], W))
            fill(R("rd", 0, EQ[3], 56), TOP)
            fill(R("rd", EQ[3], EQ[7], B), TOP)
            masks(0)
        for a, b in zip(CH, CH[1:]):
            act(R("vo", 8 * a, 8 * b), IND(R("xt"), R("sod", a // 2, b // 2)), Act.Copy)
        if first:
            waits_of(2)
        else:
            gains(n - 1, 2)
            if last:
                gains_home(2)
            elif CK:
                ensure("G", {"S": cnt["S"] - CK + 1})
                send(nxt, part("mi", 3), part("mo", 3), "ck%d" % n)
        mm(DL, R("sd"), part("mo", 0), last, False)
        mm(L0, R("se0"), part("mo", 0), False, False)
        mm(L0, R("se1"), part("mo", 0), False, True)
        if not last:
            mm(Q, R("idb"), part("mo", 3), False, False)
        halves = ((0, EARLY, BO), (EARLY, B, BE))
        for a, b, bank in halves:
            mm(R(bank, 128, 128 + b - a), R("nid"), R("zi", zo + a, zo + b), True, False)
            mm(R(BA if a else bank, 256, 256 + b - a), R("n2d"), R("zi", zo + a, zo + b), a > 0, False)
            mm(R(BA if a else bank, 256, 256 + b - a), R("idb"), R("sy", a, b), False, False)

        def places(out):
            for k in range(3):
                mm(out, R("s15"), part("mi", k), False, k == 2)
        landed("ea%d" % n, prv, R("mi", m0, m0 + mw))
        pke = PKE[core not in topo.cores_of(prv)]
        if pke >= 2:
            places(KM)
        done = [0]

        def greatest(upto):
            while done[0] < len(SC) - 1 and SC[done[0] + 1] <= upto:
                a, b = SC[done[0]], SC[done[0] + 1]
                scan(R("mx", 8 * a, 8 * b), R("r8", 0, 8 * (b - a)), R("mn2", 8 * a, 8 * b), 0.0, Op.min, Op.max)
                done[0] += 1
        for a, b in zip(CH, CH[1:]):
            tt(R("mn2", 8 * a, 8 * b), IND(R("xt"), R("sev", a // 2, b // 2)), R("vo", 8 * a, 8 * b), Op.min)
            greatest(a)
        greatest(B)
        for a, b, bank in halves:
            m = R("mx", 8 * a + 7, 8 * b, 8)
            mm(R(bank, 128, 128 + b - a), R("idb"), m, False, a > 0)
            mm(R(BA if a else bank, 256, 256 + b - a), R("idb"), m, False, True)
            act(R("s0", a, b), m, Act.Sign, -0.5)
            if a:
                keys()
            act(R("zo", zo + a, zo + b), R(bank, 128, 128 + b - a), Act.Abs)
            if a:
                send(nxt, z, R("zo", zo, zo + B), "zr%d" % n)
                if not last:
                    turn(into(1), DL)
                own_key()
                ts(R("s1", a, b), R(BA, 256, 256 + b - a), 0.5, Op.is_gt, -0.5, Op.add)
            else:
                act(R("s1", a, b), R(bank, 256, 256 + b - a), Act.Sign, -0.5)
                if pke < 2:
                    places(KM)
            mm(R(BQ, a, b), R("gn"), R("s0", a, b), last and not a, False)
            if last:
                mm(R(BQ, a, b), R("g2" if a else "gp"), R("s1", a, b), False, a > 0)
            else:
                mm(R(BQ, a, b), R("g2" if a else "gp"), R("s1", a, b), False, False)
                mm(R(BQ, a, b), R("gb"), R("zo", zo + a, zo + b), False, a > 0)
        if not last:
            turn(into(2), L0)
        ts(S7("dof0"), SEG, sc(1), Op.mult, -C0, Op.add)
        compare()
        o0 = 24 * n
        rze = not (first or last) and RZE[core not in topo.cores_of(prv)]
        landed("zr%d" % n, prv, z)

        def new_waits():
            if WDE == 2:
                tt(R("rz"), IND(R("wt", 0, W), S7("dof0")), z, Op.add)
            else:
                mm(R(BO, 0, B), R("idb"), R("wdb"), True, True)
                tt(R("rz"), z, R(BO, 0, B), Op.add)
        joint = not (first or last) and LOW[3] != "d"

        def offsets(a, b):
            ts(R("oo", o0 + a, o0 + b), R("ob", 30 + 35 * a, 31 + 35 * (b - 1), 35), 7.5 - LO, Op.add)
        if not last:
            def lows(c):
                for k in range(4):
                    if LOW[k] == c:
                        lowest(k)
            lows("a")
            ts(slot(3), slot(6), M16, Op.add, -M16, Op.add)
            lows("b")
            scan(R("ob", 275, 521, 5), R("db", 0, 50), R("pb", P0, P0 + 16 * 49 + 1, 16), 0.0, Op.mult, Op.add)
            lows("B")
            scan(R("ob", 0, 241, 5), R("da", 0, 49), R("pb", P0, P0 + 16 * 48 + 1, 16), 0.0, Op.mult, Op.add)
            lows("c")
            if rze:
                new_waits()
            offsets(0, 23 if joint else 16)
            send(nxt, R("oi", 16 * n, 16 * n + 16), R("oo", o0, o0 + 16), "of%d" % n)
            if n == 6:
                gains_home(1)
            mm(R(BQ, 128, 137), R("onb"), R("da", 2, 59, 7), True, True)
            lows("d")
        else:
            gains(n, 0)
            gains(n, 1)
            gains(n, 2)
            lowest(0)
            tt(R("fd"), R("fs"), DL, Op.mult)
            lowest(1)
            tt(R("fl"), R("fd"), L0, Op.add)
            lowest(2)
            ts(R("dt", 64, 64 + B), R("fl"), 1.0 / 32, Op.mult, -LO / 32, Op.add)
            lowest(3)
            gains_home(3)
        X1, X2 = R(BA, 0, B), R(BB, 0, B)
        if not rze:
            new_waits()
        if not joint:
            offsets(16, 23)
        ts(R("ry"), R("rz"), 31, Op.bitwise_and)
        cp(IND(R("wt"), R("oo", o0 + 16, o0 + 23)), R("ry"))
        if last:
            break
        if first or CK:
            landed("ck%d" % n, prv, part("mi", 3))
        for X in (X1, X2):
            mm(X, R("idb"), part("mi", 3), True, False)
        for X in (X1, X2):
            mm(X, R("gb"), z, False, X is X1)
        act(R("jk", 0, 9), R(BQ, 128, 137), Act.Copy, acc=R("ac", 0, 1))
        act(R("fx", 0, B), X1, Act.Identity, 14336.0, scale=-1.0)
        mm(X2, R("idb"), R("fx", 0, B), False, True)
        act(R("fa", 0, 1), R("ac", 0, 1), Act.Identity, 24.5, scale=-1.0)
        act(R("xr"), X2, Act.Identity, -14344.0)
        act(R("av", n + 1, n + 2), R("ac", 0, 1), Act.Identity, R("fa", 0, 1))
        masks(n + 1)
        gains(n, 0)

    dma("Y", T.yw[:, :], T.wt[:, 0:W], R("wt", 0, W)[1], [])
    dma("S", T.yy[:, :], T.zi[:, 8 * B:9 * B], z[1], [])
    idq = (T.idb[0:B, 0:B], R("idb")[1], [])
    for j in range(4):
        if j > 0:
            landed("tp%d" % j, cores[(rank + j) % NR], R("di", 16 * j, 16 * j + 16 if j < 3 else 64 + B))
        for h in range(2):
            a = 16 * j + 8 * h
            mm(R(BK, 0, B, p=8), R("dt" if j == 0 else "di", a, a + 8, p=B), idq, a == 0, a == 56)
    act(R("fy"), R("di", 64, 64 + B), Act.Copy)
    dma("S", T.yl[:, :], T.fy[0:128:16, :], R("fy")[1], [])
    tt(R("ft", p=8), R("tki", p=8), R(BK, 0, B, p=8), Op.add)
    ts(R("fu", p=8), R("ft", p=8), 4095, Op.bitwise_and)
    cp(R("fv", p=8), R("fu", p=8))
    dma("Y", T.yt[:, :], T.fv[0:8, :], R("fv")[1], [])
    for q in ("V", "S", "P", "G"):
        g.wait_ge(T.sem[sems[q]], cnt[q])
    for name in dma_all:
        g.wait_ge(T.sem[name], 16)
    g.wait_ge(T.sem.lsem, sent[0])
